import numpy as np
import ml_dtypes


def mxq(x, axis, fmt="e4m3"):
    dtype, down = {"e4m3": (ml_dtypes.float8_e4m3fn, 7), "e5m2": (ml_dtypes.float8_e5m2, 14)}[fmt]
    v = np.moveaxis(np.asarray(x, np.float32).astype(ml_dtypes.bfloat16).astype(np.float64), axis, -1)
    blocks = v.reshape(v.shape[:-1] + (-1, 32))
    amax = np.abs(blocks).max(-1, keepdims=True)
    byte = np.maximum(np.where(amax > 0, np.frexp(amax)[1] - 1 + 127, 0) - down, 1)
    scale = np.exp2(byte - 127.0)
    codes = (blocks / scale).astype(np.float32).astype(dtype).astype(np.float64)
    return np.moveaxis((codes * scale).reshape(v.shape), -1, axis)


WIDE = False


def mx_kscale(k):
    if not WIDE:
        return np.ones(k)
    levels = np.array([10, -10, 5, -5, 0])
    if k % 512:
        return np.exp2(np.random.permutation(np.resize(levels, k // 32))).repeat(32)
    a = np.empty((k // 512, 16))
    for p in range(k // 512):
        a[p, :8] = np.random.permutation(np.resize(levels, 8))
        for g in range(8):
            far = levels[np.abs(levels - a[p, g]) >= 10]
            a[p, g + 8] = far[np.random.randint(len(far))]
    return np.exp2(a.ravel()).repeat(32)


def f64(x):
    return np.asarray(x).astype(np.float64)


def striped(idx):
    return np.tile(np.asarray(idx).reshape(-1, 16).T, (8, 1)).astype(np.uint16)


def unstriped(offs):
    return offs[:16].T.reshape(-1).astype(np.int64)


E2M1 = np.array([0.0, 0.5, 1.0, 1.5, 2.0, 3.0, 4.0, 6.0, -0.0, -0.5, -1.0, -1.5, -2.0, -3.0, -4.0, -6.0])


def pack_weight(w, fmt):
    k, n = w.shape
    w = f64(np.asarray(w, np.float32).astype(ml_dtypes.bfloat16)).reshape(k // 32, 32, n)
    amax = np.abs(w).max(1)
    if fmt == "e4m3":
        byte = np.frexp(amax)[1] - 1 + 127 - 7
    else:
        mant, ex = np.frexp(amax / 6.0)
        byte = np.where(mant > 0.5, ex, ex - 1) + 127
    byte = np.clip(np.where(amax > 0, byte, 1), 1, 254)
    scaled = (w * np.exp2(127.0 - byte)[:, None, :]).reshape(k, n).astype(np.float32)
    by_word = np.ascontiguousarray(scaled.reshape(k // 512, 128, 4, n).transpose(0, 1, 3, 2))
    if fmt == "e4m3":
        words = by_word.astype(ml_dtypes.float8_e4m3fn).view(np.uint8)
    else:
        c = by_word.astype(ml_dtypes.float4_e2m1fn).view(np.uint8) & 0xF
        words = (c[..., 0::2] | (c[..., 1::2] << 4)).reshape(k // 512, 128, 2 * n)
    return np.ascontiguousarray(words), np.ascontiguousarray(byte.astype(np.uint8).reshape(k // 512, 16, n))


def unpack_weight(words, scales, fmt):
    g, _, n = scales.shape
    words = np.ascontiguousarray(words).reshape(g, 128, n, -1)
    if fmt == "e4m3":
        vals = words.view(ml_dtypes.float8_e4m3fn).astype(np.float64)
    else:
        nib = np.empty((g, 128, n, 4), np.uint8)
        nib[..., 0::2] = words & 0xF
        nib[..., 1::2] = words >> 4
        vals = E2M1[nib]
    vals = vals * np.repeat(np.exp2(scales.astype(np.float64) - 127.0), 8, axis=1)[..., None]
    return vals.transpose(0, 1, 3, 2).reshape(g * 512, n)


def softplus(v):
    return np.log(1.0 + np.exp(v))


def sigmoid(v):
    return 1.0 / (1.0 + np.exp(-v))


B, N, T, D, NQ = 1, 512, 2048, 512, 256


def setup_inputs():
    n = np.random.standard_normal
    idx = np.random.permutation(T)[:B * N]
    s = mx_kscale(D)[:, None]
    kp = pack_weight(n((D, T)) / s, "e4m3")
    return {
        "qT": (n((B, D, NQ)) * s * (1.00 / np.sqrt(D))).astype(np.float32),
        "k_words": kp[0],
        "k_scales": kp[1],
        "kb": np.tile(n(2048), (128, 1)).astype(np.float32),
        "offs": striped(idx),
    }


def reference(qT, k_words, k_scales, kb, offs):
    idx = unstriped(offs)
    pick = lambda x, which: x[:, which].reshape(x.shape[0], B, -1).transpose(1, 0, 2)
    k = unpack_weight(k_words, k_scales, "e4m3")
    kg = pick(k, idx)
    qq = mxq(f64(qT), 1, "e4m3")
    a = qq.transpose(0, 2, 1) @ kg
    y = np.square(sigmoid(a + pick(f64(kb), idx)[:, :1, :])) * softplus(a + pick(f64(kb), idx)[:, :1, :])
    return y

@@ -1,0 +1,152 @@
+from contextlib import ExitStack
+
+import concourse.mybir as mybir
+from concourse.masks import make_identity
+
+F32 = mybir.dt.float32
+BF16 = mybir.dt.bfloat16
+I32 = mybir.dt.int32
+U32 = mybir.dt.uint32
+U16 = mybir.dt.uint16
+U8 = mybir.dt.uint8
+FP8X4 = mybir.dt.float8_e4m3fn_x4
+ACT = mybir.ActivationFunctionType
+ALU = mybir.AluOpType
+
+P = 128
+PACK = 4
+D, T, NQ, N = 512, 2048, 256, 512
+BLOCKS = N // P
+HALVES = NQ // P
+PAIR = 2 * P
+CAP = 16.0
+BIAS_ROW = 8
+
+FLOPS = 2 * D * NQ * N
+BYTES = 4 * D * NQ + D * T + 16 * T + 4 * T + 2 * P * (N // 16) + 4 * NQ * N
+
+
+def tile_attend_link_focal_topk_kernel(tc, qT, k_words, k_scales, kb, offs, out):
+    nc = tc.nc
+    with ExitStack() as ctx:
+        sb = ctx.enter_context(tc.tile_pool(name="sb", bufs=1))
+        ps = ctx.enter_context(tc.psum_pool(name="ps", bufs=1))
+
+        offsets = sb.tile([P, N // 16], U16, name="offsets")
+        scale_pool = sb.tile([P, T], U8, name="scale_pool")
+        bias_pool = sb.tile([P, T], F32, name="bias_pool")
+        word_pool = sb.tile([P, T], I32, name="word_pool")
+        q_raw = sb.tile([P, PACK, NQ], F32, name="q_raw")
+        cap_col = sb.tile([P, 1], F32, name="cap_col")
+        floor_col = sb.tile([P, 1], F32, name="floor_col")
+        ident = sb.tile([P, P], F32, name="ident")
+
+        nc.vector.memset(scale_pool[:].bitcast(I32), 0)
+        nc.vector.memset(cap_col[:], -CAP)
+        nc.vector.memset(bias_pool[:].bitcast(I32), 0)
+        make_identity(nc, ident[:])
+
+        words_dram = k_words[0].rearrange("p t r -> p (t r)").bitcast(I32)
+        scales_dram = k_scales[0].bitcast(I32)
+        nc.sync.dma_start(offsets[:], offs)
+        for quad in range(4):
+            nc.scalar.dma_start(
+                scale_pool[:].bitcast(I32)[32 * quad : 32 * quad + 4, :],
+                scales_dram[4 * quad : 4 * quad + 4, :],
+            )
+        nc.sync.dma_start(q_raw[:], qT[0].rearrange("(p j) w -> p j w", j=PACK))
+        nc.sync.dma_start(word_pool[:, : T // 2], words_dram[:, : T // 2])
+        nc.sync.dma_start(bias_pool[BIAS_ROW : BIAS_ROW + 1, :], kb[BIAS_ROW : BIAS_ROW + 1, :])
+        nc.sync.dma_start(word_pool[:, T // 2 :], words_dram[:, T // 2 :])
+
+        nc.scalar.activation(floor_col[:], cap_col[:], ACT.Sigmoid)
+
+        k_sc = sb.tile([P, N], U8, name="k_sc", align_bytes=64)
+        nc.vector.tensor_copy(k_sc[:], scale_pool[:].indirect(offsets[:]))
+        bias_g = sb.tile([P, N], F32, name="bias_g")
+        nc.vector.tensor_copy(bias_g[:], bias_pool[:].indirect(offsets[:]))
+
+        q_bf = sb.tile([P, NQ, PACK], BF16, name="q_bf", align_bytes=64)
+        nc.scalar.activation(q_bf[:], q_raw[:].rearrange("p j w -> p w j"), ACT.Copy, scale=-1.0 / CAP)
+        q_codes = sb.tile([P, NQ], U32, name="q_codes", align_bytes=64)
+        q_sc = sb.tile([P, NQ], U8, name="q_sc", align_bytes=64)
+        nc.vector.quantize_mx(
+            out=q_codes[:].bitcast(FP8X4), scales=q_sc[:], in_=q_bf[:].rearrange("p w j -> p (w j)")
+        )
+
+        bias_t = ps.tile([P, BLOCKS, P], F32, name="bias_t", tag="n_t1")
+        for j in range(BLOCKS):
+            nc.tensor.transpose(bias_t[:, j, :], bias_g[:, j * P : (j + 1) * P], ident[:])
+        neg_b = sb.tile([P, BLOCKS], F32, name="neg_b")
+        one_less_b = sb.tile([P, BLOCKS], F32, name="one_less_b")
+        nc.scalar.activation(neg_b[:], bias_t[:, :, BIAS_ROW], ACT.Copy, scale=-1.0)
+        nc.scalar.activation(one_less_b[:], bias_t[:, :, BIAS_ROW], ACT.Copy, scale=-1.0 / CAP, bias=1.0)
+
+        k_codes = []
+        for c in range(2):
+            codes = sb.tile([P, PAIR], U32, name="k_codes%d" % c, align_bytes=64)
+            nc.vector.tensor_copy(
+                codes[:], word_pool[:].bitcast(U32).indirect(offsets[:, 16 * c : 16 * (c + 1)])
+            )
+            k_codes.append(codes)
+
+        scores = []
+        for j in range(BLOCKS):
+            acc = ps.tile([P, NQ], F32, name="scores%d" % j)
+            nc.tensor.matmul_mx(
+                out=acc[:],
+                lhsT=k_codes[j // 2][:, (j % 2) * P : (j % 2 + 1) * P].bitcast(FP8X4),
+                lhsT_scale=k_sc[:, j * P : (j + 1) * P],
+                rhs=q_codes[:].bitcast(FP8X4),
+                rhs_scale=q_sc[:],
+                start=True,
+                stop=True,
+            )
+            scores.append(acc)
+
+        m = [sb.tile([P, 2, NQ], F32, name="m%d" % c) for c in range(2)]
+        for j in range(BLOCKS):
+            nc.scalar.activation(
+                m[j // 2][:, j % 2, :], scores[j][:], ACT.Sigmoid, bias=neg_b[:, j : j + 1], scale=CAP
+            )
+
+        w = [sb.tile([P, 2, NQ], F32, name="w%d" % c) for c in range(2)]
+        hn = [sb.tile([P, 2, NQ], F32, name="hn%d" % c) for c in range(2)]
+        nn = [sb.tile([P, 2, NQ], F32, name="nn%d" % c) for c in range(2)]
+        w_t = [ps.tile([P, HALVES, PAIR], F32, name="w_t%d" % c) for c in range(2)]
+        n_t = [ps.tile([P, HALVES, PAIR], F32, name="n_t%d" % c, tag="n_t%d" % c) for c in range(2)]
+
+        def turn(dst, src):
+            for i in range(2):
+                for h in range(HALVES):
+                    nc.tensor.transpose(dst[:, h, i * P : (i + 1) * P], src[:, i, h * P : (h + 1) * P], ident[:])
+
+        def clamp(c):
+            nc.vector.tensor_scalar(w[c][:], m[c][:], floor_col[:], -1.0, ALU.max, ALU.mult)
+            turn(w_t[c], w[c])
+
+        def square(c):
+            nc.vector.scalar_tensor_tensor(hn[c][:], m[c][:], 2.0, w[c][:], ALU.subtract, ALU.mult)
+
+        def factor(c):
+            for i in range(2):
+                j = 2 * c + i
+                nc.vector.scalar_tensor_tensor(
+                    nn[c][:, i, :], scores[j][:], one_less_b[:, j : j + 1], hn[c][:, i, :], ALU.add, ALU.min
+                )
+            turn(n_t[c], nn[c])
+
+        clamp(0)
+        square(0)
+        clamp(1)
+        factor(0)
+        square(1)
+        factor(1)
+
+        out_v = out[0].rearrange("(h p) n -> p h n", p=P)
+        for c in range(2):
+            logs = sb.tile([P, HALVES, PAIR], F32, name="logs%d" % c)
+            nc.scalar.activation(logs[:], w_t[c][:], ACT.Ln, scale=-1.0)
+            y = sb.tile([P, HALVES, PAIR], F32, name="y%d" % c)
+            nc.vector.scalar_tensor_tensor(y[:], n_t[c][:], 1.0, logs[:], ALU.subtract, ALU.mult)
+            nc.sync.dma_start(out_v[:, :, c * PAIR : (c + 1) * PAIR], y[:])

@@ -33,33 +33,32 @@ def tile_attend_link_focal_topk_kernel(tc, qT, k_words, k_scales, kb, offs, out)
         ps = ctx.enter_context(tc.psum_pool(name="ps", bufs=1))
 
         offsets = sb.tile([P, N // 16], U16, name="offsets")
-        scale_pool = sb.tile([P, T], U8, name="scale_pool")
-        bias_pool = sb.tile([P, T], F32, name="bias_pool")
-        word_pool = sb.tile([P, T], I32, name="word_pool")
+        scale_pool = sb.tile([P, T], U8, name="scale_pool", tag="scale_bytes", align_bytes=64)
+        bias_pool = sb.tile([P, T], F32, name="bias_pool", tag="reused", align_bytes=64)
         q_raw = sb.tile([P, PACK, NQ], F32, name="q_raw")
-        cap_col = sb.tile([P, 1], F32, name="cap_col")
+        cap_col = sb.tile([P, 1], F32, name="cap_col", tag="cap_then_words")
         floor_col = sb.tile([P, 1], F32, name="floor_col")
         ident = sb.tile([P, P], F32, name="ident")
 
         nc.vector.memset(scale_pool[:].bitcast(I32), 0)
-        nc.vector.memset(cap_col[:], -CAP)
         nc.vector.memset(bias_pool[:].bitcast(I32), 0)
-        make_identity(nc, ident[:])
+        nc.vector.memset(cap_col[:], -CAP)
+        nc.vector.memset(ident[:], 0.0)
+        make_identity(nc, ident[:], nomemset=True)
 
         words_dram = k_words[0].rearrange("p t r -> p (t r)").bitcast(I32)
         scales_dram = k_scales[0].bitcast(I32)
         nc.sync.dma_start(offsets[:], offs)
+        nc.sync.dma_start(q_raw[:], qT[0].rearrange("(p j) w -> p j w", j=PACK))
         for quad in range(4):
-            nc.scalar.dma_start(
+            nc.sync.dma_start(
                 scale_pool[:].bitcast(I32)[32 * quad : 32 * quad + 4, :],
                 scales_dram[4 * quad : 4 * quad + 4, :],
             )
-        nc.sync.dma_start(q_raw[:], qT[0].rearrange("(p j) w -> p j w", j=PACK))
-        nc.sync.dma_start(word_pool[:, : T // 2], words_dram[:, : T // 2])
         nc.sync.dma_start(bias_pool[BIAS_ROW : BIAS_ROW + 1, :], kb[BIAS_ROW : BIAS_ROW + 1, :])
-        nc.sync.dma_start(word_pool[:, T // 2 :], words_dram[:, T // 2 :])
-
         nc.scalar.activation(floor_col[:], cap_col[:], ACT.Sigmoid)
+        word_pool = sb.tile([P, T], I32, name="word_pool", tag="cap_then_words")
+        nc.sync.dma_start(word_pool[:], words_dram)
 
         k_sc = sb.tile([P, N], U8, name="k_sc", align_bytes=64)
         nc.vector.tensor_copy(k_sc[:], scale_pool[:].indirect(offsets[:]))
@@ -69,7 +68,7 @@ def tile_attend_link_focal_topk_kernel(tc, qT, k_words, k_scales, kb, offs, out)
         q_bf = sb.tile([P, NQ, PACK], BF16, name="q_bf", align_bytes=64)
         nc.scalar.activation(q_bf[:], q_raw[:].rearrange("p j w -> p w j"), ACT.Copy, scale=-1.0 / CAP)
         q_codes = sb.tile([P, NQ], U32, name="q_codes", align_bytes=64)
-        q_sc = sb.tile([P, NQ], U8, name="q_sc", align_bytes=64)
+        q_sc = sb.tile([P, NQ], U8, name="q_sc", tag="scale_bytes", align_bytes=64)
         nc.vector.quantize_mx(
             out=q_codes[:].bitcast(FP8X4), scales=q_sc[:], in_=q_bf[:].rearrange("p w j -> p (w j)")
         )
@@ -82,20 +81,19 @@ def tile_attend_link_focal_topk_kernel(tc, qT, k_words, k_scales, kb, offs, out)
         nc.scalar.activation(neg_b[:], bias_t[:, :, BIAS_ROW], ACT.Copy, scale=-1.0)
         nc.scalar.activation(one_less_b[:], bias_t[:, :, BIAS_ROW], ACT.Copy, scale=-1.0 / CAP, bias=1.0)
 
-        k_codes = []
+        k_codes = sb.tile([P, N], U32, name="k_codes", tag="reused", align_bytes=64)
         for c in range(2):
-            codes = sb.tile([P, PAIR], U32, name="k_codes%d" % c, align_bytes=64)
             nc.vector.tensor_copy(
-                codes[:], word_pool[:].bitcast(U32).indirect(offsets[:, 16 * c : 16 * (c + 1)])
+                k_codes[:, c * PAIR : (c + 1) * PAIR],
+                word_pool[:].bitcast(U32).indirect(offsets[:, 16 * c : 16 * (c + 1)]),
             )
-            k_codes.append(codes)
 
         scores = []
         for j in range(BLOCKS):
-            acc = ps.tile([P, NQ], F32, name="scores%d" % j)
+            acc = ps.tile([P, NQ], F32, name="scores%d" % j, tag="scores%d" % j)
             nc.tensor.matmul_mx(
                 out=acc[:],
-                lhsT=k_codes[j // 2][:, (j % 2) * P : (j % 2 + 1) * P].bitcast(FP8X4),
+                lhsT=k_codes[:, j * P : (j + 1) * P].bitcast(FP8X4),
                 lhsT_scale=k_sc[:, j * P : (j + 1) * P],
                 rhs=q_codes[:].bitcast(FP8X4),
                 rhs_scale=q_sc[:],
@@ -114,7 +112,8 @@ def tile_attend_link_focal_topk_kernel(tc, qT, k_words, k_scales, kb, offs, out)
         hn = [sb.tile([P, 2, NQ], F32, name="hn%d" % c) for c in range(2)]
         nn = [sb.tile([P, 2, NQ], F32, name="nn%d" % c) for c in range(2)]
         w_t = [ps.tile([P, HALVES, PAIR], F32, name="w_t%d" % c) for c in range(2)]
-        n_t = [ps.tile([P, HALVES, PAIR], F32, name="n_t%d" % c, tag="n_t%d" % c) for c in range(2)]
+        pieces = [(0, 2, "n_t0"), (2, 1, "n_t1"), (3, 1, "scores0")]
+        n_t = {}
 
         def turn(dst, src):
             for i in range(2):
@@ -128,25 +127,35 @@ def tile_attend_link_focal_topk_kernel(tc, qT, k_words, k_scales, kb, offs, out)
         def square(c):
             nc.vector.scalar_tensor_tensor(hn[c][:], m[c][:], 2.0, w[c][:], ALU.subtract, ALU.mult)
 
-        def factor(c):
-            for i in range(2):
-                j = 2 * c + i
-                nc.vector.scalar_tensor_tensor(
-                    nn[c][:, i, :], scores[j][:], one_less_b[:, j : j + 1], hn[c][:, i, :], ALU.add, ALU.min
-                )
-            turn(n_t[c], nn[c])
+        def factor(j):
+            c, i = divmod(j, 2)
+            nc.vector.scalar_tensor_tensor(
+                nn[c][:, i, :], scores[j][:], one_less_b[:, j : j + 1], hn[c][:, i, :], ALU.add, ALU.min
+            )
+            for first, count, tag in pieces:
+                if j == first:
+                    n_t[first] = ps.tile([P, HALVES, count * P], F32, name="n_t%d" % first, tag=tag)
+                if first <= j < first + count:
+                    cols = slice((j - first) * P, (j - first + 1) * P)
+                    for h in range(HALVES):
+                        nc.tensor.transpose(n_t[first][:, h, cols], nn[c][:, i, h * P : (h + 1) * P], ident[:])
 
         clamp(0)
         square(0)
         clamp(1)
         factor(0)
         square(1)
-        factor(1)
+        for j in range(1, BLOCKS):
+            factor(j)
 
         out_v = out[0].rearrange("(h p) n -> p h n", p=P)
+        logs = [sb.tile([P, HALVES, PAIR], F32, name="logs%d" % c) for c in range(2)]
         for c in range(2):
-            logs = sb.tile([P, HALVES, PAIR], F32, name="logs%d" % c)
-            nc.scalar.activation(logs[:], w_t[c][:], ACT.Ln, scale=-1.0)
-            y = sb.tile([P, HALVES, PAIR], F32, name="y%d" % c)
-            nc.vector.scalar_tensor_tensor(y[:], n_t[c][:], 1.0, logs[:], ALU.subtract, ALU.mult)
-            nc.sync.dma_start(out_v[:, :, c * PAIR : (c + 1) * PAIR], y[:])
+            nc.scalar.activation(logs[c][:], w_t[c][:], ACT.Ln, scale=-1.0)
+        for first, count, tag in pieces:
+            c, i = divmod(first, 2)
+            y = sb.tile([P, HALVES, count * P], F32, name="y%d" % first)
+            nc.vector.scalar_tensor_tensor(
+                y[:], n_t[first][:], 1.0, logs[c][:, :, i * P : (i + count) * P], ALU.subtract, ALU.mult
+            )
+            nc.sync.dma_start(out_v[:, :, first * P : (first + count) * P], y[:])

@@ -21,6 +21,7 @@ HALVES = NQ // P
 PAIR = 2 * P
 CAP = 16.0
 BIAS_ROW = 8
+EARLY = 512
 
 FLOPS = 2 * D * NQ * N
 BYTES = 4 * D * NQ + D * T + 16 * T + 4 * T + 2 * P * (N // 16) + 4 * NQ * N
@@ -30,35 +31,37 @@ def tile_attend_link_focal_topk_kernel(tc, qT, k_words, k_scales, kb, offs, out)
     nc = tc.nc
     with ExitStack() as ctx:
         sb = ctx.enter_context(tc.tile_pool(name="sb", bufs=1))
+        overlay = ctx.enter_context(tc.tile_pool(name="overlay", bufs=1))
         ps = ctx.enter_context(tc.psum_pool(name="ps", bufs=1))
 
         offsets = sb.tile([P, N // 16], U16, name="offsets")
-        scale_pool = sb.tile([P, T], U8, name="scale_pool", tag="scale_bytes", align_bytes=64)
-        bias_pool = sb.tile([P, T], F32, name="bias_pool", tag="reused", align_bytes=64)
+        scale_pool = sb.tile([P, T], U8, name="scale_pool")
+        bias_pool = overlay.tile([P, T], F32, name="bias_pool", align_bytes=64, offset=0)
+        word_pool = sb.tile([P, T], I32, name="word_pool")
         q_raw = sb.tile([P, PACK, NQ], F32, name="q_raw")
-        cap_col = sb.tile([P, 1], F32, name="cap_col", tag="cap_then_words")
+        cap_col = sb.tile([P, 1], F32, name="cap_col")
         floor_col = sb.tile([P, 1], F32, name="floor_col")
         ident = sb.tile([P, P], F32, name="ident")
 
         nc.vector.memset(scale_pool[:].bitcast(I32), 0)
         nc.vector.memset(bias_pool[:].bitcast(I32), 0)
-        nc.vector.memset(cap_col[:], -CAP)
+        nc.gpsimd.memset(cap_col[:], -CAP)
         nc.vector.memset(ident[:], 0.0)
         make_identity(nc, ident[:], nomemset=True)
 
         words_dram = k_words[0].rearrange("p t r -> p (t r)").bitcast(I32)
         scales_dram = k_scales[0].bitcast(I32)
         nc.sync.dma_start(offsets[:], offs)
-        nc.sync.dma_start(q_raw[:], qT[0].rearrange("(p j) w -> p j w", j=PACK))
+        nc.sync.dma_start(word_pool[:, :EARLY], words_dram[:, :EARLY])
         for quad in range(4):
             nc.sync.dma_start(
                 scale_pool[:].bitcast(I32)[32 * quad : 32 * quad + 4, :],
                 scales_dram[4 * quad : 4 * quad + 4, :],
             )
+        nc.sync.dma_start(q_raw[:], qT[0].rearrange("(p j) w -> p j w", j=PACK))
         nc.sync.dma_start(bias_pool[BIAS_ROW : BIAS_ROW + 1, :], kb[BIAS_ROW : BIAS_ROW + 1, :])
+        nc.sync.dma_start(word_pool[:, EARLY:], words_dram[:, EARLY:])
         nc.scalar.activation(floor_col[:], cap_col[:], ACT.Sigmoid)
-        word_pool = sb.tile([P, T], I32, name="word_pool", tag="cap_then_words")
-        nc.sync.dma_start(word_pool[:], words_dram)
 
         k_sc = sb.tile([P, N], U8, name="k_sc", align_bytes=64)
         nc.vector.tensor_copy(k_sc[:], scale_pool[:].indirect(offsets[:]))
@@ -68,7 +71,7 @@ def tile_attend_link_focal_topk_kernel(tc, qT, k_words, k_scales, kb, offs, out)
         q_bf = sb.tile([P, NQ, PACK], BF16, name="q_bf", align_bytes=64)
         nc.scalar.activation(q_bf[:], q_raw[:].rearrange("p j w -> p w j"), ACT.Copy, scale=-1.0 / CAP)
         q_codes = sb.tile([P, NQ], U32, name="q_codes", align_bytes=64)
-        q_sc = sb.tile([P, NQ], U8, name="q_sc", tag="scale_bytes", align_bytes=64)
+        q_sc = overlay.tile([P, NQ], U8, name="q_sc", align_bytes=64, offset=0)
         nc.vector.quantize_mx(
             out=q_codes[:].bitcast(FP8X4), scales=q_sc[:], in_=q_bf[:].rearrange("p w j -> p (w j)")
         )
@@ -81,7 +84,7 @@ def tile_attend_link_focal_topk_kernel(tc, qT, k_words, k_scales, kb, offs, out)
         nc.scalar.activation(neg_b[:], bias_t[:, :, BIAS_ROW], ACT.Copy, scale=-1.0)
         nc.scalar.activation(one_less_b[:], bias_t[:, :, BIAS_ROW], ACT.Copy, scale=-1.0 / CAP, bias=1.0)
 
-        k_codes = sb.tile([P, N], U32, name="k_codes", tag="reused", align_bytes=64)
+        k_codes = overlay.tile([P, N], U32, name="k_codes", align_bytes=64, offset=1024)
         for c in range(2):
             nc.vector.tensor_copy(
                 k_codes[:, c * PAIR : (c + 1) * PAIR],
@@ -115,17 +118,15 @@ def tile_attend_link_focal_topk_kernel(tc, qT, k_words, k_scales, kb, offs, out)
         pieces = [(0, 2, "n_t0"), (2, 1, "n_t1"), (3, 1, "scores0")]
         n_t = {}
 
-        def turn(dst, src):
-            for i in range(2):
-                for h in range(HALVES):
-                    nc.tensor.transpose(dst[:, h, i * P : (i + 1) * P], src[:, i, h * P : (h + 1) * P], ident[:])
+        def clamp(j):
+            c, i = divmod(j, 2)
+            nc.vector.tensor_scalar(w[c][:, i, :], m[c][:, i, :], floor_col[:], -1.0, ALU.max, ALU.mult)
+            for h in range(HALVES):
+                nc.tensor.transpose(w_t[c][:, h, i * P : (i + 1) * P], w[c][:, i, h * P : (h + 1) * P], ident[:])
 
-        def clamp(c):
-            nc.vector.tensor_scalar(w[c][:], m[c][:], floor_col[:], -1.0, ALU.max, ALU.mult)
-            turn(w_t[c], w[c])
-
-        def square(c):
-            nc.vector.scalar_tensor_tensor(hn[c][:], m[c][:], 2.0, w[c][:], ALU.subtract, ALU.mult)
+        def square(j):
+            c, i = divmod(j, 2)
+            nc.vector.scalar_tensor_tensor(hn[c][:, i, :], m[c][:, i, :], 2.0, w[c][:, i, :], ALU.subtract, ALU.mult)
 
         def factor(j):
             c, i = divmod(j, 2)
@@ -140,13 +141,13 @@ def tile_attend_link_focal_topk_kernel(tc, qT, k_words, k_scales, kb, offs, out)
                     for h in range(HALVES):
                         nc.tensor.transpose(n_t[first][:, h, cols], nn[c][:, i, h * P : (h + 1) * P], ident[:])
 
-        clamp(0)
-        square(0)
-        clamp(1)
-        factor(0)
-        square(1)
-        for j in range(1, BLOCKS):
-            factor(j)
+        for step in range(BLOCKS + 2):
+            if step < BLOCKS:
+                clamp(step)
+            if 0 <= step - 1 < BLOCKS:
+                square(step - 1)
+            if 0 <= step - 2 < BLOCKS:
+                factor(step - 2)
 
         out_v = out[0].rearrange("(h p) n -> p h n", p=P)
         logs = [sb.tile([P, HALVES, PAIR], F32, name="logs%d" % c) for c in range(2)]

@@ -1,7 +1,6 @@
 from contextlib import ExitStack
 
 import concourse.mybir as mybir
-from concourse.masks import make_identity
 
 F32 = mybir.dt.float32
 BF16 = mybir.dt.bfloat16
@@ -20,8 +19,8 @@ BLOCKS = N // P
 HALVES = NQ // P
 PAIR = 2 * P
 CAP = 16.0
-BIAS_ROW = 8
-EARLY = 512
+BIAS_ROW = P - 1
+AT_BIAS, AT_SCALES, AT_QBF, AT_WORDS = 0, 8192, 10240, 12288
 
 FLOPS = 2 * D * NQ * N
 BYTES = 4 * D * NQ + D * T + 16 * T + 4 * T + 2 * P * (N // 16) + 4 * NQ * N
@@ -35,43 +34,43 @@ def tile_attend_link_focal_topk_kernel(tc, qT, k_words, k_scales, kb, offs, out)
         ps = ctx.enter_context(tc.psum_pool(name="ps", bufs=1))
 
         offsets = sb.tile([P, N // 16], U16, name="offsets")
-        scale_pool = sb.tile([P, T], U8, name="scale_pool")
-        bias_pool = overlay.tile([P, T], F32, name="bias_pool", align_bytes=64, offset=0)
-        word_pool = sb.tile([P, T], I32, name="word_pool")
+        scale_pool = overlay.tile([P, T], U8, name="scale_pool", align_bytes=64, offset=AT_SCALES)
+        bias_pool = overlay.tile([P, T], F32, name="bias_pool", align_bytes=64, offset=AT_BIAS)
+        zeros = overlay.tile([P, P], F32, name="zeros", align_bytes=64, offset=AT_WORDS)
         q_raw = sb.tile([P, PACK, NQ], F32, name="q_raw")
         cap_col = sb.tile([P, 1], F32, name="cap_col")
         floor_col = sb.tile([P, 1], F32, name="floor_col")
         ident = sb.tile([P, P], F32, name="ident")
 
         nc.vector.memset(scale_pool[:].bitcast(I32), 0)
-        nc.vector.memset(bias_pool[:].bitcast(I32), 0)
+        nc.vector.memset(zeros[:], 0.0)
+        nc.vector.memset(bias_pool[:BIAS_ROW, :].bitcast(I32), 0)
         nc.gpsimd.memset(cap_col[:], -CAP)
-        nc.vector.memset(ident[:], 0.0)
-        make_identity(nc, ident[:], nomemset=True)
+        nc.gpsimd.affine_select(
+            out=ident[:], in_=zeros[:], compare_op=ALU.not_equal, fill=1.0, base=0,
+            pattern=[[-1, P]], channel_multiplier=1,
+        )
 
         words_dram = k_words[0].rearrange("p t r -> p (t r)").bitcast(I32)
         scales_dram = k_scales[0].bitcast(I32)
         nc.sync.dma_start(offsets[:], offs)
-        nc.sync.dma_start(word_pool[:, :EARLY], words_dram[:, :EARLY])
-        for quad in range(4):
-            nc.sync.dma_start(
-                scale_pool[:].bitcast(I32)[32 * quad : 32 * quad + 4, :],
-                scales_dram[4 * quad : 4 * quad + 4, :],
-            )
+        nc.sync.dma_start(bias_pool[BIAS_ROW:, :], kb[BIAS_ROW:, :])
         nc.sync.dma_start(q_raw[:], qT[0].rearrange("(p j) w -> p j w", j=PACK))
-        nc.sync.dma_start(bias_pool[BIAS_ROW : BIAS_ROW + 1, :], kb[BIAS_ROW : BIAS_ROW + 1, :])
-        nc.sync.dma_start(word_pool[:, EARLY:], words_dram[:, EARLY:])
+        for r in range(4):
+            nc.sync.dma_start(scale_pool[:].bitcast(I32)[r:P:32, :], scales_dram[r:16:4, :])
+        word_pool = overlay.tile([P, T], I32, name="word_pool", align_bytes=64, offset=AT_WORDS)
+        nc.sync.dma_start(word_pool[:], words_dram)
         nc.scalar.activation(floor_col[:], cap_col[:], ACT.Sigmoid)
 
-        k_sc = sb.tile([P, N], U8, name="k_sc", align_bytes=64)
-        nc.vector.tensor_copy(k_sc[:], scale_pool[:].indirect(offsets[:]))
         bias_g = sb.tile([P, N], F32, name="bias_g")
         nc.vector.tensor_copy(bias_g[:], bias_pool[:].indirect(offsets[:]))
+        k_sc = overlay.tile([P, N], U8, name="k_sc", align_bytes=64, offset=AT_BIAS)
+        nc.vector.tensor_copy(k_sc[:], scale_pool[:].indirect(offsets[:]))
 
-        q_bf = sb.tile([P, NQ, PACK], BF16, name="q_bf", align_bytes=64)
+        q_bf = overlay.tile([P, NQ, PACK], BF16, name="q_bf", align_bytes=64, offset=AT_QBF)
         nc.scalar.activation(q_bf[:], q_raw[:].rearrange("p j w -> p w j"), ACT.Copy, scale=-1.0 / CAP)
         q_codes = sb.tile([P, NQ], U32, name="q_codes", align_bytes=64)
-        q_sc = overlay.tile([P, NQ], U8, name="q_sc", align_bytes=64, offset=0)
+        q_sc = overlay.tile([P, NQ], U8, name="q_sc", align_bytes=64, offset=AT_SCALES)
         nc.vector.quantize_mx(
             out=q_codes[:].bitcast(FP8X4), scales=q_sc[:], in_=q_bf[:].rearrange("p w j -> p (w j)")
         )
@@ -84,7 +83,7 @@ def tile_attend_link_focal_topk_kernel(tc, qT, k_words, k_scales, kb, offs, out)
         nc.scalar.activation(neg_b[:], bias_t[:, :, BIAS_ROW], ACT.Copy, scale=-1.0)
         nc.scalar.activation(one_less_b[:], bias_t[:, :, BIAS_ROW], ACT.Copy, scale=-1.0 / CAP, bias=1.0)
 
-        k_codes = overlay.tile([P, N], U32, name="k_codes", align_bytes=64, offset=1024)
+        k_codes = overlay.tile([P, N], U32, name="k_codes", align_bytes=64, offset=AT_QBF)
         for c in range(2):
             nc.vector.tensor_copy(
                 k_codes[:, c * PAIR : (c + 1) * PAIR],

@@ -1,6 +1,7 @@
 from contextlib import ExitStack
 
 import concourse.mybir as mybir
+from concourse.masks import make_identity
 
 F32 = mybir.dt.float32
 BF16 = mybir.dt.bfloat16
@@ -20,7 +21,7 @@ HALVES = NQ // P
 PAIR = 2 * P
 CAP = 16.0
 BIAS_ROW = P - 1
-AT_BIAS, AT_SCALES, AT_QBF, AT_WORDS = 0, 8192, 10240, 12288
+AT_BIAS, AT_SCALES, AT_QBF = 0, 8192, 10240
 
 FLOPS = 2 * D * NQ * N
 BYTES = 4 * D * NQ + D * T + 16 * T + 4 * T + 2 * P * (N // 16) + 4 * NQ * N
@@ -36,20 +37,17 @@ def tile_attend_link_focal_topk_kernel(tc, qT, k_words, k_scales, kb, offs, out)
         offsets = sb.tile([P, N // 16], U16, name="offsets")
         scale_pool = overlay.tile([P, T], U8, name="scale_pool", align_bytes=64, offset=AT_SCALES)
         bias_pool = overlay.tile([P, T], F32, name="bias_pool", align_bytes=64, offset=AT_BIAS)
-        zeros = overlay.tile([P, P], F32, name="zeros", align_bytes=64, offset=AT_WORDS)
+        word_pool = sb.tile([P, T], I32, name="word_pool")
         q_raw = sb.tile([P, PACK, NQ], F32, name="q_raw")
         cap_col = sb.tile([P, 1], F32, name="cap_col")
         floor_col = sb.tile([P, 1], F32, name="floor_col")
         ident = sb.tile([P, P], F32, name="ident")
 
         nc.vector.memset(scale_pool[:].bitcast(I32), 0)
-        nc.vector.memset(zeros[:], 0.0)
         nc.vector.memset(bias_pool[:BIAS_ROW, :].bitcast(I32), 0)
+        nc.vector.memset(ident[:], 0.0)
         nc.gpsimd.memset(cap_col[:], -CAP)
-        nc.gpsimd.affine_select(
-            out=ident[:], in_=zeros[:], compare_op=ALU.not_equal, fill=1.0, base=0,
-            pattern=[[-1, P]], channel_multiplier=1,
-        )
+        make_identity(nc, ident[:], nomemset=True)
 
         words_dram = k_words[0].rearrange("p t r -> p (t r)").bitcast(I32)
         scales_dram = k_scales[0].bitcast(I32)
@@ -58,7 +56,6 @@ def tile_attend_link_focal_topk_kernel(tc, qT, k_words, k_scales, kb, offs, out)
         nc.sync.dma_start(q_raw[:], qT[0].rearrange("(p j) w -> p j w", j=PACK))
         for r in range(4):
             nc.sync.dma_start(scale_pool[:].bitcast(I32)[r:P:32, :], scales_dram[r:16:4, :])
-        word_pool = overlay.tile([P, T], I32, name="word_pool", align_bytes=64, offset=AT_WORDS)
         nc.sync.dma_start(word_pool[:], words_dram)
         nc.scalar.activation(floor_col[:], cap_col[:], ACT.Sigmoid)
 
@@ -114,7 +111,6 @@ def tile_attend_link_focal_topk_kernel(tc, qT, k_words, k_scales, kb, offs, out)
         hn = [sb.tile([P, 2, NQ], F32, name="hn%d" % c) for c in range(2)]
         nn = [sb.tile([P, 2, NQ], F32, name="nn%d" % c) for c in range(2)]
         w_t = [ps.tile([P, HALVES, PAIR], F32, name="w_t%d" % c) for c in range(2)]
-        pieces = [(0, 2, "n_t0"), (2, 1, "n_t1"), (3, 1, "scores0")]
         n_t = {}
 
         def clamp(j):
@@ -132,13 +128,17 @@ def tile_attend_link_focal_topk_kernel(tc, qT, k_words, k_scales, kb, offs, out)
             nc.vector.scalar_tensor_tensor(
                 nn[c][:, i, :], scores[j][:], one_less_b[:, j : j + 1], hn[c][:, i, :], ALU.add, ALU.min
             )
-            for first, count, tag in pieces:
-                if j == first:
-                    n_t[first] = ps.tile([P, HALVES, count * P], F32, name="n_t%d" % first, tag=tag)
-                if first <= j < first + count:
-                    cols = slice((j - first) * P, (j - first + 1) * P)
-                    for h in range(HALVES):
-                        nc.tensor.transpose(n_t[first][:, h, cols], nn[c][:, i, h * P : (h + 1) * P], ident[:])
+            if j == 0:
+                n_t[0] = ps.tile([P, HALVES, PAIR], F32, name="n_t0", tag="n_t0")
+            if j == 2:
+                n_t[2] = ps.tile([P, HALVES, P], F32, name="n_t2", tag="n_t1")
+            for h in range(HALVES):
+                if j == 3:
+                    n_t[3, h] = ps.tile([P, P], F32, name="n_t3%d" % h, tag="scores%d" % h)
+                    dst = n_t[3, h][:]
+                else:
+                    dst = n_t[2 * c][:, h, i * P : (i + 1) * P]
+                nc.tensor.transpose(dst, nn[c][:, i, h * P : (h + 1) * P], ident[:])
 
         for step in range(BLOCKS + 2):
             if step < BLOCKS:
@@ -149,13 +149,22 @@ def tile_attend_link_focal_topk_kernel(tc, qT, k_words, k_scales, kb, offs, out)
                 factor(step - 2)
 
         out_v = out[0].rearrange("(h p) n -> p h n", p=P)
-        logs = [sb.tile([P, HALVES, PAIR], F32, name="logs%d" % c) for c in range(2)]
-        for c in range(2):
-            nc.scalar.activation(logs[c][:], w_t[c][:], ACT.Ln, scale=-1.0)
-        for first, count, tag in pieces:
-            c, i = divmod(first, 2)
-            y = sb.tile([P, HALVES, count * P], F32, name="y%d" % first)
-            nc.vector.scalar_tensor_tensor(
-                y[:], n_t[first][:], 1.0, logs[c][:, :, i * P : (i + count) * P], ALU.subtract, ALU.mult
-            )
-            nc.sync.dma_start(out_v[:, :, first * P : (first + count) * P], y[:])
+
+        def log_of(name, src, shape):
+            logs = sb.tile(shape, F32, name="logs" + name)
+            nc.scalar.activation(logs[:], src, ACT.Ln, scale=-1.0)
+            return logs
+
+        def finish(name, n_src, logs, dst, shape):
+            y = sb.tile(shape, F32, name="y" + name)
+            nc.vector.scalar_tensor_tensor(y[:], n_src, 1.0, logs, ALU.subtract, ALU.mult)
+            nc.sync.dma_start(dst, y[:])
+
+        for h in range(HALVES):
+            logs = log_of("0%d" % h, w_t[0][:, h, :], [P, PAIR])
+            finish("0%d" % h, n_t[0][:, h, :], logs[:], out_v[:, h, :PAIR], [P, PAIR])
+        logs = log_of("2", w_t[1][:, :, :P], [P, HALVES, P])
+        finish("2", n_t[2][:], logs[:], out_v[:, :, 2 * P : 3 * P], [P, HALVES, P])
+        logs = log_of("3", w_t[1][:, :, P:], [P, HALVES, P])
+        for h in range(HALVES):
+            finish("3%d" % h, n_t[3, h][:], logs[:, h, :], out_v[:, h, 3 * P :], [P, P])

@@ -41,12 +41,14 @@ def tile_attend_link_focal_topk_kernel(tc, qT, k_words, k_scales, kb, offs, out)
         q_raw = sb.tile([P, PACK, NQ], F32, name="q_raw")
         cap_col = sb.tile([P, 1], F32, name="cap_col")
         floor_col = sb.tile([P, 1], F32, name="floor_col")
+        tiny_col = sb.tile([P, 1], F32, name="tiny_col")
         ident = sb.tile([P, P], F32, name="ident")
 
         nc.vector.memset(scale_pool[:].bitcast(I32), 0)
-        nc.vector.memset(bias_pool[:BIAS_ROW, :].bitcast(I32), 0)
+        nc.vector.memset(bias_pool[:BIAS_ROW, : T // 2].bitcast(I32), 0)
         nc.vector.memset(ident[:], 0.0)
         nc.gpsimd.memset(cap_col[:], -CAP)
+        nc.gpsimd.memset(bias_pool[:BIAS_ROW, T // 2 :].bitcast(I32), 0)
         make_identity(nc, ident[:], nomemset=True)
 
         words_dram = k_words[0].rearrange("p t r -> p (t r)").bitcast(I32)
@@ -58,6 +60,7 @@ def tile_attend_link_focal_topk_kernel(tc, qT, k_words, k_scales, kb, offs, out)
             nc.sync.dma_start(scale_pool[:].bitcast(I32)[r:P:32, :], scales_dram[r:16:4, :])
         nc.sync.dma_start(word_pool[:], words_dram)
         nc.scalar.activation(floor_col[:], cap_col[:], ACT.Sigmoid)
+        nc.scalar.activation(tiny_col[:], floor_col[:], ACT.Square)
 
         bias_g = sb.tile([P, N], F32, name="bias_g")
         nc.vector.tensor_copy(bias_g[:], bias_pool[:].indirect(offsets[:]))
@@ -76,9 +79,20 @@ def tile_attend_link_focal_topk_kernel(tc, qT, k_words, k_scales, kb, offs, out)
         for j in range(BLOCKS):
             nc.tensor.transpose(bias_t[:, j, :], bias_g[:, j * P : (j + 1) * P], ident[:])
         neg_b = sb.tile([P, BLOCKS], F32, name="neg_b")
-        one_less_b = sb.tile([P, BLOCKS], F32, name="one_less_b")
+        knee = sb.tile([P, BLOCKS], F32, name="knee")
+        seed = sb.tile([P, BLOCKS], F32, name="seed")
+        nc.scalar.activation(seed[:], bias_t[:, :, BIAS_ROW], ACT.Copy, scale=-1.0 / CAP)
         nc.scalar.activation(neg_b[:], bias_t[:, :, BIAS_ROW], ACT.Copy, scale=-1.0)
-        nc.scalar.activation(one_less_b[:], bias_t[:, :, BIAS_ROW], ACT.Copy, scale=-1.0 / CAP, bias=1.0)
+        nc.scalar.activation(knee[:], bias_t[:, :, BIAS_ROW], ACT.Copy, scale=1.0 / CAP, bias=-1.0)
+
+        n_t = [ps.tile([P, HALVES, PAIR], F32, name="n_t%d" % c, tag="n_t%d" % c) for c in range(2)]
+        for j in range(BLOCKS):
+            c, i = divmod(j, 2)
+            for h in range(HALVES):
+                nc.tensor.matmul(
+                    n_t[c][:, h, i * P : (i + 1) * P], seed[:, j : j + 1].to_broadcast([P, P]), ident[:],
+                    start=(i == 0 and h == 0), stop=False, is_transpose=True,
+                )
 
         k_codes = overlay.tile([P, N], U32, name="k_codes", align_bytes=64, offset=AT_QBF)
         for c in range(2):
@@ -101,70 +115,43 @@ def tile_attend_link_focal_topk_kernel(tc, qT, k_words, k_scales, kb, offs, out)
             )
             scores.append(acc)
 
-        m = [sb.tile([P, 2, NQ], F32, name="m%d" % c) for c in range(2)]
+        m = [sb.tile([P, NQ], F32, name="m%d" % j) for j in range(BLOCKS)]
+        hn = [sb.tile([P, NQ], F32, name="hn%d" % j) for j in range(BLOCKS)]
+        nn = [sb.tile([P, NQ], F32, name="nn%d" % j) for j in range(BLOCKS)]
+        m_t = [ps.tile([P, HALVES, PAIR], F32, name="m_t%d" % c) for c in range(2)]
         for j in range(BLOCKS):
-            nc.scalar.activation(
-                m[j // 2][:, j % 2, :], scores[j][:], ACT.Sigmoid, bias=neg_b[:, j : j + 1], scale=CAP
-            )
-
-        w = [sb.tile([P, 2, NQ], F32, name="w%d" % c) for c in range(2)]
-        hn = [sb.tile([P, 2, NQ], F32, name="hn%d" % c) for c in range(2)]
-        nn = [sb.tile([P, 2, NQ], F32, name="nn%d" % c) for c in range(2)]
-        w_t = [ps.tile([P, HALVES, PAIR], F32, name="w_t%d" % c) for c in range(2)]
-        n_t = {}
-
-        def clamp(j):
             c, i = divmod(j, 2)
-            nc.vector.tensor_scalar(w[c][:, i, :], m[c][:, i, :], floor_col[:], -1.0, ALU.max, ALU.mult)
+            nc.scalar.activation(m[j][:], scores[j][:], ACT.Sigmoid, bias=neg_b[:, j : j + 1], scale=CAP)
             for h in range(HALVES):
-                nc.tensor.transpose(w_t[c][:, h, i * P : (i + 1) * P], w[c][:, i, h * P : (h + 1) * P], ident[:])
+                nc.tensor.transpose(m_t[c][:, h, i * P : (i + 1) * P], m[j][:, h * P : (h + 1) * P], ident[:])
 
         def square(j):
-            c, i = divmod(j, 2)
-            nc.vector.scalar_tensor_tensor(hn[c][:, i, :], m[c][:, i, :], 2.0, w[c][:, i, :], ALU.subtract, ALU.mult)
+            nc.vector.scalar_tensor_tensor(hn[j][:], m[j][:], 2.0, m[j][:], ALU.subtract, ALU.mult)
 
         def factor(j):
             c, i = divmod(j, 2)
             nc.vector.scalar_tensor_tensor(
-                nn[c][:, i, :], scores[j][:], one_less_b[:, j : j + 1], hn[c][:, i, :], ALU.add, ALU.min
+                nn[j][:], scores[j][:], knee[:, j : j + 1], hn[j][:], ALU.min, ALU.subtract
             )
-            if j == 0:
-                n_t[0] = ps.tile([P, HALVES, PAIR], F32, name="n_t0", tag="n_t0")
-            if j == 2:
-                n_t[2] = ps.tile([P, HALVES, P], F32, name="n_t2", tag="n_t1")
             for h in range(HALVES):
-                if j == 3:
-                    n_t[3, h] = ps.tile([P, P], F32, name="n_t3%d" % h, tag="scores%d" % h)
-                    dst = n_t[3, h][:]
-                else:
-                    dst = n_t[2 * c][:, h, i * P : (i + 1) * P]
-                nc.tensor.transpose(dst, nn[c][:, i, h * P : (h + 1) * P], ident[:])
+                nc.tensor.matmul(
+                    n_t[c][:, h, i * P : (i + 1) * P], nn[j][:, h * P : (h + 1) * P], ident[:],
+                    start=False, stop=(i == 1 and h == HALVES - 1), is_transpose=True,
+                )
 
-        for step in range(BLOCKS + 2):
+        for step in range(BLOCKS + 1):
             if step < BLOCKS:
-                clamp(step)
-            if 0 <= step - 1 < BLOCKS:
-                square(step - 1)
-            if 0 <= step - 2 < BLOCKS:
-                factor(step - 2)
+                square(step)
+            if step >= 1:
+                factor(step - 1)
 
-        out_v = out[0].rearrange("(h p) n -> p h n", p=P)
-
-        def log_of(name, src, shape):
-            logs = sb.tile(shape, F32, name="logs" + name)
-            nc.scalar.activation(logs[:], src, ACT.Ln, scale=-1.0)
-            return logs
-
-        def finish(name, n_src, logs, dst, shape):
-            y = sb.tile(shape, F32, name="y" + name)
-            nc.vector.scalar_tensor_tensor(y[:], n_src, 1.0, logs, ALU.subtract, ALU.mult)
-            nc.sync.dma_start(dst, y[:])
-
-        for h in range(HALVES):
-            logs = log_of("0%d" % h, w_t[0][:, h, :], [P, PAIR])
-            finish("0%d" % h, n_t[0][:, h, :], logs[:], out_v[:, h, :PAIR], [P, PAIR])
-        logs = log_of("2", w_t[1][:, :, :P], [P, HALVES, P])
-        finish("2", n_t[2][:], logs[:], out_v[:, :, 2 * P : 3 * P], [P, HALVES, P])
-        logs = log_of("3", w_t[1][:, :, P:], [P, HALVES, P])
-        for h in range(HALVES):
-            finish("3%d" % h, n_t[3, h][:], logs[:, h, :], out_v[:, h, 3 * P :], [P, P])
+        ends = [(0, 0, 0, P), (0, 0, P, P), (0, 1, 0, PAIR), (1, 0, 0, PAIR), (1, 1, 0, P), (1, 1, P, P)]
+        for e, (c, h, first, width) in enumerate(ends):
+            logs = sb.tile([P, width], F32, name="logs%d" % e)
+            nc.scalar.activation(logs[:], m_t[c][:, h, first : first + width], ACT.Ln, bias=tiny_col[:])
+            y = sb.tile([P, width], F32, name="y%d" % e)
+            nc.vector.scalar_tensor_tensor(
+                y[:], logs[:], -CAP, n_t[c][:, h, first : first + width], ALU.max, ALU.mult
+            )
+            col = c * PAIR + first
+            nc.sync.dma_start(out[0, h * P : (h + 1) * P, col : col + width], y[:])

@@ -45,10 +45,9 @@ def tile_attend_link_focal_topk_kernel(tc, qT, k_words, k_scales, kb, offs, out)
         ident = sb.tile([P, P], F32, name="ident")
 
         nc.vector.memset(scale_pool[:].bitcast(I32), 0)
-        nc.vector.memset(bias_pool[:BIAS_ROW, : T // 2].bitcast(I32), 0)
+        nc.vector.memset(bias_pool[:BIAS_ROW, :].bitcast(I32), 0)
         nc.vector.memset(ident[:], 0.0)
         nc.gpsimd.memset(cap_col[:], -CAP)
-        nc.gpsimd.memset(bias_pool[:BIAS_ROW, T // 2 :].bitcast(I32), 0)
         make_identity(nc, ident[:], nomemset=True)
 
         words_dram = k_words[0].rearrange("p t r -> p (t r)").bitcast(I32)

@@ -21,7 +21,6 @@ HALVES = NQ // P
 PAIR = 2 * P
 CAP = 16.0
 BIAS_ROW = P - 1
-AT_BIAS, AT_SCALES, AT_QBF = 0, 8192, 10240
 
 FLOPS = 2 * D * NQ * N
 BYTES = 4 * D * NQ + D * T + 16 * T + 4 * T + 2 * P * (N // 16) + 4 * NQ * N
@@ -35,8 +34,8 @@ def tile_attend_link_focal_topk_kernel(tc, qT, k_words, k_scales, kb, offs, out)
         ps = ctx.enter_context(tc.psum_pool(name="ps", bufs=1))
 
         offsets = sb.tile([P, N // 16], U16, name="offsets")
-        scale_pool = overlay.tile([P, T], U8, name="scale_pool", align_bytes=64, offset=AT_SCALES)
-        bias_pool = overlay.tile([P, T], F32, name="bias_pool", align_bytes=64, offset=AT_BIAS)
+        scale_pool = overlay.tile([P, T], U8, name="scale_pool", align_bytes=64, offset=0)
+        bias_pool = sb.tile([P, T], F32, name="bias_pool")
         word_pool = sb.tile([P, T], I32, name="word_pool")
         q_raw = sb.tile([P, PACK, NQ], F32, name="q_raw")
         cap_col = sb.tile([P, 1], F32, name="cap_col")
@@ -63,13 +62,18 @@ def tile_attend_link_focal_topk_kernel(tc, qT, k_words, k_scales, kb, offs, out)
 
         bias_g = sb.tile([P, N], F32, name="bias_g")
         nc.vector.tensor_copy(bias_g[:], bias_pool[:].indirect(offsets[:]))
-        k_sc = overlay.tile([P, N], U8, name="k_sc", align_bytes=64, offset=AT_BIAS)
+        k_sc = sb.tile([P, N], U8, name="k_sc", align_bytes=64)
         nc.vector.tensor_copy(k_sc[:], scale_pool[:].indirect(offsets[:]))
 
-        q_bf = overlay.tile([P, NQ, PACK], BF16, name="q_bf", align_bytes=64, offset=AT_QBF)
-        nc.scalar.activation(q_bf[:], q_raw[:].rearrange("p j w -> p w j"), ACT.Copy, scale=-1.0 / CAP)
+        q_bf = sb.tile([P, NQ, PACK], BF16, name="q_bf", align_bytes=64)
+        nc.scalar.activation(
+            q_bf[:].rearrange("p (c i) j -> p c j i", i=PACK),
+            q_raw[:].rearrange("p j (c i) -> p c j i", i=PACK),
+            ACT.Copy,
+            scale=-1.0 / CAP,
+        )
         q_codes = sb.tile([P, NQ], U32, name="q_codes", align_bytes=64)
-        q_sc = overlay.tile([P, NQ], U8, name="q_sc", align_bytes=64, offset=AT_SCALES)
+        q_sc = overlay.tile([P, NQ], U8, name="q_sc", align_bytes=64, offset=0)
         nc.vector.quantize_mx(
             out=q_codes[:].bitcast(FP8X4), scales=q_sc[:], in_=q_bf[:].rearrange("p w j -> p (w j)")
         )
@@ -93,7 +97,7 @@ def tile_attend_link_focal_topk_kernel(tc, qT, k_words, k_scales, kb, offs, out)
                     start=(i == 0 and h == 0), stop=False, is_transpose=True,
                 )
 
-        k_codes = overlay.tile([P, N], U32, name="k_codes", align_bytes=64, offset=AT_QBF)
+        k_codes = overlay.tile([P, N], U32, name="k_codes", align_bytes=64, offset=NQ)
         for c in range(2):
             nc.vector.tensor_copy(
                 k_codes[:, c * PAIR : (c + 1) * PAIR],

@@ -30,11 +30,10 @@ def tile_attend_link_focal_topk_kernel(tc, qT, k_words, k_scales, kb, offs, out)
     nc = tc.nc
     with ExitStack() as ctx:
         sb = ctx.enter_context(tc.tile_pool(name="sb", bufs=1))
-        overlay = ctx.enter_context(tc.tile_pool(name="overlay", bufs=1))
         ps = ctx.enter_context(tc.psum_pool(name="ps", bufs=1))
 
         offsets = sb.tile([P, N // 16], U16, name="offsets")
-        scale_pool = overlay.tile([P, T], U8, name="scale_pool", align_bytes=64, offset=0)
+        scale_pool = sb.tile([P, T], U8, name="scale_pool", align_bytes=64)
         bias_pool = sb.tile([P, T], F32, name="bias_pool")
         word_pool = sb.tile([P, T], I32, name="word_pool")
         q_raw = sb.tile([P, PACK, NQ], F32, name="q_raw")
@@ -42,28 +41,33 @@ def tile_attend_link_focal_topk_kernel(tc, qT, k_words, k_scales, kb, offs, out)
         floor_col = sb.tile([P, 1], F32, name="floor_col")
         tiny_col = sb.tile([P, 1], F32, name="tiny_col")
         ident = sb.tile([P, P], F32, name="ident")
+        k_sc = sb.tile([P, N], U8, name="k_sc", align_bytes=64)
 
-        nc.vector.memset(scale_pool[:].bitcast(I32), 0)
+        nc.vector.memset(scale_pool[:48, :].bitcast(I32), 0)
+        nc.vector.memset(scale_pool[64:, :].bitcast(I32), 0)
         nc.vector.memset(bias_pool[:BIAS_ROW, :].bitcast(I32), 0)
         nc.vector.memset(ident[:], 0.0)
         nc.gpsimd.memset(cap_col[:], -CAP)
+        nc.gpsimd.memset(k_sc[:].bitcast(I32), 0)
         make_identity(nc, ident[:], nomemset=True)
 
         words_dram = k_words[0].rearrange("p t r -> p (t r)").bitcast(I32)
         scales_dram = k_scales[0].bitcast(I32)
         nc.sync.dma_start(offsets[:], offs)
+        nc.sync.dma_start(scale_pool[:].bitcast(I32)[48:64, :], scales_dram)
         nc.sync.dma_start(bias_pool[BIAS_ROW:, :], kb[BIAS_ROW:, :])
         nc.sync.dma_start(q_raw[:], qT[0].rearrange("(p j) w -> p j w", j=PACK))
-        for r in range(4):
-            nc.sync.dma_start(scale_pool[:].bitcast(I32)[r:P:32, :], scales_dram[r:16:4, :])
         nc.sync.dma_start(word_pool[:], words_dram)
         nc.scalar.activation(floor_col[:], cap_col[:], ACT.Sigmoid)
         nc.scalar.activation(tiny_col[:], floor_col[:], ACT.Square)
 
-        bias_g = sb.tile([P, N], F32, name="bias_g")
-        nc.vector.tensor_copy(bias_g[:], bias_pool[:].indirect(offsets[:]))
-        k_sc = sb.tile([P, N], U8, name="k_sc", align_bytes=64)
-        nc.vector.tensor_copy(k_sc[:], scale_pool[:].indirect(offsets[:]))
+        scale_g = sb.tile([P, N], U8, name="scale_g", align_bytes=64)
+        nc.vector.tensor_copy(scale_g[:], scale_pool[:].indirect(offsets[:]))
+        for r in range(4):
+            nc.sync.dma_start(k_sc[:].bitcast(I32)[r:P:32, :], scale_g[:].bitcast(I32)[48 + r : 64 : 4, :])
+        bias_g = [sb.tile([P, PAIR], F32, name="bias_g%d" % c) for c in range(2)]
+        for c in range(2):
+            nc.vector.tensor_copy(bias_g[c][:], bias_pool[:].indirect(offsets[:, 16 * c : 16 * (c + 1)]))
 
         q_bf = sb.tile([P, NQ, PACK], BF16, name="q_bf", align_bytes=64)
         nc.scalar.activation(
@@ -73,31 +77,38 @@ def tile_attend_link_focal_topk_kernel(tc, qT, k_words, k_scales, kb, offs, out)
             scale=-1.0 / CAP,
         )
         q_codes = sb.tile([P, NQ], U32, name="q_codes", align_bytes=64)
-        q_sc = overlay.tile([P, NQ], U8, name="q_sc", align_bytes=64, offset=0)
+        q_sc = sb.tile([P, NQ], U8, name="q_sc", align_bytes=64)
         nc.vector.quantize_mx(
             out=q_codes[:].bitcast(FP8X4), scales=q_sc[:], in_=q_bf[:].rearrange("p w j -> p (w j)")
         )
 
-        bias_t = ps.tile([P, BLOCKS, P], F32, name="bias_t", tag="n_t1")
-        for j in range(BLOCKS):
-            nc.tensor.transpose(bias_t[:, j, :], bias_g[:, j * P : (j + 1) * P], ident[:])
+        bias_t = [ps.tile([P, 2, P], F32, name="bias_t%d" % c, tag="m_t%d" % c) for c in range(2)]
         neg_b = sb.tile([P, BLOCKS], F32, name="neg_b")
         knee = sb.tile([P, BLOCKS], F32, name="knee")
         seed = sb.tile([P, BLOCKS], F32, name="seed")
-        nc.scalar.activation(seed[:], bias_t[:, :, BIAS_ROW], ACT.Copy, scale=-1.0 / CAP)
-        nc.scalar.activation(neg_b[:], bias_t[:, :, BIAS_ROW], ACT.Copy, scale=-1.0)
-        nc.scalar.activation(knee[:], bias_t[:, :, BIAS_ROW], ACT.Copy, scale=1.0 / CAP, bias=-1.0)
+        for c in range(2):
+            for i in range(2):
+                nc.tensor.transpose(bias_t[c][:, i, :], bias_g[c][:, i * P : (i + 1) * P], ident[:])
+        for c in range(2):
+            nc.scalar.activation(seed[:, 2 * c : 2 * c + 2], bias_t[c][:, :, BIAS_ROW], ACT.Copy, scale=-1.0 / CAP)
+        nc.scalar.activation(neg_b[:], seed[:], ACT.Copy, scale=CAP)
+        nc.scalar.activation(knee[:], seed[:], ACT.Copy, scale=-1.0, bias=-1.0)
 
-        n_t = [ps.tile([P, HALVES, PAIR], F32, name="n_t%d" % c, tag="n_t%d" % c) for c in range(2)]
-        for j in range(BLOCKS):
-            c, i = divmod(j, 2)
-            for h in range(HALVES):
-                nc.tensor.matmul(
-                    n_t[c][:, h, i * P : (i + 1) * P], seed[:, j : j + 1].to_broadcast([P, P]), ident[:],
-                    start=(i == 0 and h == 0), stop=False, is_transpose=True,
-                )
+        n_t = []
 
-        k_codes = overlay.tile([P, N], U32, name="k_codes", align_bytes=64, offset=NQ)
+        def seed_bank(c, tag):
+            bank = ps.tile([P, HALVES, PAIR], F32, name="n_t%d" % c, tag=tag)
+            for i in range(2):
+                for h in range(HALVES):
+                    nc.tensor.matmul(
+                        bank[:, h, i * P : (i + 1) * P], seed[:, 2 * c + i : 2 * c + i + 1].to_broadcast([P, P]),
+                        ident[:], start=(i == 0 and h == 0), stop=False, is_transpose=True,
+                    )
+            n_t.append(bank)
+
+        seed_bank(0, "n_t0")
+
+        k_codes = sb.tile([P, N], U32, name="k_codes", align_bytes=64)
         for c in range(2):
             nc.vector.tensor_copy(
                 k_codes[:, c * PAIR : (c + 1) * PAIR],
@@ -121,7 +132,7 @@ def tile_attend_link_focal_topk_kernel(tc, qT, k_words, k_scales, kb, offs, out)
         m = [sb.tile([P, NQ], F32, name="m%d" % j) for j in range(BLOCKS)]
         hn = [sb.tile([P, NQ], F32, name="hn%d" % j) for j in range(BLOCKS)]
         nn = [sb.tile([P, NQ], F32, name="nn%d" % j) for j in range(BLOCKS)]
-        m_t = [ps.tile([P, HALVES, PAIR], F32, name="m_t%d" % c) for c in range(2)]
+        m_t = [ps.tile([P, HALVES, PAIR], F32, name="m_t%d" % c, tag="m_t%d" % c) for c in range(2)]
         for j in range(BLOCKS):
             c, i = divmod(j, 2)
             nc.scalar.activation(m[j][:], scores[j][:], ACT.Sigmoid, bias=neg_b[:, j : j + 1], scale=CAP)
@@ -147,6 +158,8 @@ def tile_attend_link_focal_topk_kernel(tc, qT, k_words, k_scales, kb, offs, out)
                 square(step)
             if step >= 1:
                 factor(step - 1)
+            if step == 1:
+                seed_bank(1, "scores0")
 
         ends = [(0, 0, 0, P), (0, 0, P, P), (0, 1, 0, PAIR), (1, 0, 0, PAIR), (1, 1, 0, P), (1, 1, P, P)]
         for e, (c, h, first, width) in enumerate(ends):

@@ -54,7 +54,7 @@ def tile_attend_link_focal_topk_kernel(tc, qT, k_words, k_scales, kb, offs, out)
         words_dram = k_words[0].rearrange("p t r -> p (t r)").bitcast(I32)
         scales_dram = k_scales[0].bitcast(I32)
         nc.sync.dma_start(offsets[:], offs)
-        nc.sync.dma_start(scale_pool[:].bitcast(I32)[48:64, :], scales_dram)
+        nc.scalar.dma_start(scale_pool[:].bitcast(I32)[48:64, :], scales_dram)
         nc.sync.dma_start(bias_pool[BIAS_ROW:, :], kb[BIAS_ROW:, :])
         nc.sync.dma_start(q_raw[:], qT[0].rearrange("(p j) w -> p j w", j=PACK))
         nc.sync.dma_start(word_pool[:], words_dram)
@@ -91,7 +91,7 @@ def tile_attend_link_focal_topk_kernel(tc, qT, k_words, k_scales, kb, offs, out)
                 nc.tensor.transpose(bias_t[c][:, i, :], bias_g[c][:, i * P : (i + 1) * P], ident[:])
         for c in range(2):
             nc.scalar.activation(seed[:, 2 * c : 2 * c + 2], bias_t[c][:, :, BIAS_ROW], ACT.Copy, scale=-1.0 / CAP)
-        nc.scalar.activation(neg_b[:], seed[:], ACT.Copy, scale=CAP)
+            nc.scalar.activation(neg_b[:, 2 * c : 2 * c + 2], bias_t[c][:, :, BIAS_ROW], ACT.Copy, scale=-1.0)
         nc.scalar.activation(knee[:], seed[:], ACT.Copy, scale=-1.0, bias=-1.0)
 
         n_t = []
@@ -115,15 +115,16 @@ def tile_attend_link_focal_topk_kernel(tc, qT, k_words, k_scales, kb, offs, out)
                 word_pool[:].bitcast(U32).indirect(offsets[:, 16 * c : 16 * (c + 1)]),
             )
 
+        parts = [(0, 0, P), (0, P, P)] + [(j, 0, NQ) for j in range(1, BLOCKS)]
         scores = []
-        for j in range(BLOCKS):
-            acc = ps.tile([P, NQ], F32, name="scores%d" % j, tag="scores%d" % j)
+        for u, (j, first, width) in enumerate(parts):
+            acc = ps.tile([P, width], F32, name="scores%d" % u, tag="scores%d" % u)
             nc.tensor.matmul_mx(
                 out=acc[:],
                 lhsT=k_codes[:, j * P : (j + 1) * P].bitcast(FP8X4),
                 lhsT_scale=k_sc[:, j * P : (j + 1) * P],
-                rhs=q_codes[:].bitcast(FP8X4),
-                rhs_scale=q_sc[:],
+                rhs=q_codes[:, first : first + width].bitcast(FP8X4),
+                rhs_scale=q_sc[:, first : first + width],
                 start=True,
                 stop=True,
             )
@@ -133,9 +134,12 @@ def tile_attend_link_focal_topk_kernel(tc, qT, k_words, k_scales, kb, offs, out)
         hn = [sb.tile([P, NQ], F32, name="hn%d" % j) for j in range(BLOCKS)]
         nn = [sb.tile([P, NQ], F32, name="nn%d" % j) for j in range(BLOCKS)]
         m_t = [ps.tile([P, HALVES, PAIR], F32, name="m_t%d" % c, tag="m_t%d" % c) for c in range(2)]
+        for u, (j, first, width) in enumerate(parts):
+            nc.scalar.activation(
+                m[j][:, first : first + width], scores[u][:], ACT.Sigmoid, bias=neg_b[:, j : j + 1], scale=CAP
+            )
         for j in range(BLOCKS):
             c, i = divmod(j, 2)
-            nc.scalar.activation(m[j][:], scores[j][:], ACT.Sigmoid, bias=neg_b[:, j : j + 1], scale=CAP)
             for h in range(HALVES):
                 nc.tensor.transpose(m_t[c][:, h, i * P : (i + 1) * P], m[j][:, h * P : (h + 1) * P], ident[:])
 
@@ -144,9 +148,12 @@ def tile_attend_link_focal_topk_kernel(tc, qT, k_words, k_scales, kb, offs, out)
 
         def factor(j):
             c, i = divmod(j, 2)
-            nc.vector.scalar_tensor_tensor(
-                nn[j][:], scores[j][:], knee[:, j : j + 1], hn[j][:], ALU.min, ALU.subtract
-            )
+            for u, (block, first, width) in enumerate(parts):
+                if block == j:
+                    nc.vector.scalar_tensor_tensor(
+                        nn[j][:, first : first + width], scores[u][:], knee[:, j : j + 1],
+                        hn[j][:, first : first + width], ALU.min, ALU.subtract,
+                    )
             for h in range(HALVES):
                 nc.tensor.matmul(
                     n_t[c][:, h, i * P : (i + 1) * P], nn[j][:, h * P : (h + 1) * P], ident[:],

@@ -53,9 +53,9 @@ def tile_attend_link_focal_topk_kernel(tc, qT, k_words, k_scales, kb, offs, out)
 
         words_dram = k_words[0].rearrange("p t r -> p (t r)").bitcast(I32)
         scales_dram = k_scales[0].bitcast(I32)
-        nc.sync.dma_start(offsets[:], offs)
-        nc.scalar.dma_start(scale_pool[:].bitcast(I32)[48:64, :], scales_dram)
         nc.sync.dma_start(bias_pool[BIAS_ROW:, :], kb[BIAS_ROW:, :])
+        nc.scalar.dma_start(scale_pool[:].bitcast(I32)[48:64, :], scales_dram)
+        nc.sync.dma_start(offsets[:], offs)
         nc.sync.dma_start(q_raw[:], qT[0].rearrange("(p j) w -> p j w", j=PACK))
         nc.sync.dma_start(word_pool[:], words_dram)
         nc.scalar.activation(floor_col[:], cap_col[:], ACT.Sigmoid)

@@ -168,7 +168,7 @@ def tile_attend_link_focal_topk_kernel(tc, qT, k_words, k_scales, kb, offs, out)
             if step == 1:
                 seed_bank(1, "scores0")
 
-        ends = [(0, 0, 0, P), (0, 0, P, P), (0, 1, 0, PAIR), (1, 0, 0, PAIR), (1, 1, 0, P), (1, 1, P, P)]
+        ends = [(c, h, 0, PAIR) for c in range(2) for h in range(HALVES)]
         for e, (c, h, first, width) in enumerate(ends):
             logs = sb.tile([P, width], F32, name="logs%d" % e)
             nc.scalar.activation(logs[:], m_t[c][:, h, first : first + width], ACT.Ln, bias=tiny_col[:])

@@ -19,11 +19,17 @@ D, T, NQ, N = 512, 2048, 256, 512
 BLOCKS = N // P
 HALVES = NQ // P
 PAIR = 2 * P
+PAIRS = N // PAIR
+PAIR_COLS = PAIR // 16
+SCALE_ROWS = D // 32
+QUADRANT = 32
+GROUP = SCALE_ROWS * QUADRANT // P
 CAP = 16.0
 BIAS_ROW = P - 1
+SCALE_FIRST = P - SCALE_ROWS
 
 FLOPS = 2 * D * NQ * N
-BYTES = 4 * D * NQ + D * T + 16 * T + 4 * T + 2 * P * (N // 16) + 4 * NQ * N
+BYTES = 4 * D * NQ + D * T + SCALE_ROWS * T + 4 * T + 2 * P * (N // 16) + 4 * NQ * N
 
 
 def tile_attend_link_focal_topk_kernel(tc, qT, k_words, k_scales, kb, offs, out):
@@ -43,31 +49,37 @@ def tile_attend_link_focal_topk_kernel(tc, qT, k_words, k_scales, kb, offs, out)
         ident = sb.tile([P, P], F32, name="ident")
         k_sc = sb.tile([P, N], U8, name="k_sc", align_bytes=64)
 
-        nc.vector.memset(scale_pool[:48, :].bitcast(I32), 0)
-        nc.vector.memset(scale_pool[64:, :].bitcast(I32), 0)
+        nc.vector.memset(scale_pool[:SCALE_FIRST, :].bitcast(I32), 0)
         nc.vector.memset(bias_pool[:BIAS_ROW, :].bitcast(I32), 0)
         nc.vector.memset(ident[:], 0.0)
         nc.gpsimd.memset(cap_col[:], -CAP)
-        nc.gpsimd.memset(k_sc[:].bitcast(I32), 0)
+        nc.vector.memset(k_sc[:].bitcast(I32), 0)
         make_identity(nc, ident[:], nomemset=True)
 
         words_dram = k_words[0].rearrange("p t r -> p (t r)").bitcast(I32)
         scales_dram = k_scales[0].bitcast(I32)
-        nc.sync.dma_start(bias_pool[BIAS_ROW:, :], kb[BIAS_ROW:, :])
-        nc.scalar.dma_start(scale_pool[:].bitcast(I32)[48:64, :], scales_dram)
         nc.sync.dma_start(offsets[:], offs)
+        nc.scalar.dma_start(scale_pool[:].bitcast(I32)[SCALE_FIRST:, :], scales_dram)
+        nc.sync.dma_start(bias_pool[BIAS_ROW:, :], kb[BIAS_ROW:, :])
         nc.sync.dma_start(q_raw[:], qT[0].rearrange("(p j) w -> p j w", j=PACK))
         nc.sync.dma_start(word_pool[:], words_dram)
+
         nc.scalar.activation(floor_col[:], cap_col[:], ACT.Sigmoid)
         nc.scalar.activation(tiny_col[:], floor_col[:], ACT.Square)
 
         scale_g = sb.tile([P, N], U8, name="scale_g", align_bytes=64)
         nc.vector.tensor_copy(scale_g[:], scale_pool[:].indirect(offsets[:]))
-        for r in range(4):
-            nc.sync.dma_start(k_sc[:].bitcast(I32)[r:P:32, :], scale_g[:].bitcast(I32)[48 + r : 64 : 4, :])
-        bias_g = [sb.tile([P, PAIR], F32, name="bias_g%d" % c) for c in range(2)]
-        for c in range(2):
-            nc.vector.tensor_copy(bias_g[c][:], bias_pool[:].indirect(offsets[:, 16 * c : 16 * (c + 1)]))
+        for r in range(GROUP):
+            nc.sync.dma_start(
+                k_sc[:].bitcast(I32)[r:P:QUADRANT, :],
+                scale_g[:].bitcast(I32)[SCALE_FIRST + r : SCALE_FIRST + SCALE_ROWS : GROUP, :],
+            )
+
+        bias_g = [sb.tile([P, PAIR], F32, name="bias_g%d" % c) for c in range(PAIRS)]
+        for c in range(PAIRS):
+            nc.vector.tensor_copy(
+                bias_g[c][:], bias_pool[:].indirect(offsets[:, PAIR_COLS * c : PAIR_COLS * (c + 1)])
+            )
 
         q_bf = sb.tile([P, NQ, PACK], BF16, name="q_bf", align_bytes=64)
         nc.scalar.activation(
@@ -82,14 +94,14 @@ def tile_attend_link_focal_topk_kernel(tc, qT, k_words, k_scales, kb, offs, out)
             out=q_codes[:].bitcast(FP8X4), scales=q_sc[:], in_=q_bf[:].rearrange("p w j -> p (w j)")
         )
 
-        bias_t = [ps.tile([P, 2, P], F32, name="bias_t%d" % c, tag="m_t%d" % c) for c in range(2)]
+        bias_t = [ps.tile([P, 2, P], F32, name="bias_t%d" % c, tag="m_t%d" % c) for c in range(PAIRS)]
         neg_b = sb.tile([P, BLOCKS], F32, name="neg_b")
         knee = sb.tile([P, BLOCKS], F32, name="knee")
         seed = sb.tile([P, BLOCKS], F32, name="seed")
-        for c in range(2):
+        for c in range(PAIRS):
             for i in range(2):
                 nc.tensor.transpose(bias_t[c][:, i, :], bias_g[c][:, i * P : (i + 1) * P], ident[:])
-        for c in range(2):
+        for c in range(PAIRS):
             nc.scalar.activation(seed[:, 2 * c : 2 * c + 2], bias_t[c][:, :, BIAS_ROW], ACT.Copy, scale=-1.0 / CAP)
             nc.scalar.activation(neg_b[:, 2 * c : 2 * c + 2], bias_t[c][:, :, BIAS_ROW], ACT.Copy, scale=-1.0)
         nc.scalar.activation(knee[:], seed[:], ACT.Copy, scale=-1.0, bias=-1.0)
@@ -109,10 +121,10 @@ def tile_attend_link_focal_topk_kernel(tc, qT, k_words, k_scales, kb, offs, out)
         seed_bank(0, "n_t0")
 
         k_codes = sb.tile([P, N], U32, name="k_codes", align_bytes=64)
-        for c in range(2):
+        for c in range(PAIRS):
             nc.vector.tensor_copy(
                 k_codes[:, c * PAIR : (c + 1) * PAIR],
-                word_pool[:].bitcast(U32).indirect(offsets[:, 16 * c : 16 * (c + 1)]),
+                word_pool[:].bitcast(U32).indirect(offsets[:, PAIR_COLS * c : PAIR_COLS * (c + 1)]),
             )
 
         parts = [(0, 0, P), (0, P, P)] + [(j, 0, NQ) for j in range(1, BLOCKS)]
@@ -133,7 +145,7 @@ def tile_attend_link_focal_topk_kernel(tc, qT, k_words, k_scales, kb, offs, out)
         m = [sb.tile([P, NQ], F32, name="m%d" % j) for j in range(BLOCKS)]
         hn = [sb.tile([P, NQ], F32, name="hn%d" % j) for j in range(BLOCKS)]
         nn = [sb.tile([P, NQ], F32, name="nn%d" % j) for j in range(BLOCKS)]
-        m_t = [ps.tile([P, HALVES, PAIR], F32, name="m_t%d" % c, tag="m_t%d" % c) for c in range(2)]
+        m_t = [ps.tile([P, HALVES, PAIR], F32, name="m_t%d" % c, tag="m_t%d" % c) for c in range(PAIRS)]
         for u, (j, first, width) in enumerate(parts):
             nc.scalar.activation(
                 m[j][:, first : first + width], scores[u][:], ACT.Sigmoid, bias=neg_b[:, j : j + 1], scale=CAP
@@ -160,21 +172,18 @@ def tile_attend_link_focal_topk_kernel(tc, qT, k_words, k_scales, kb, offs, out)
                     start=False, stop=(i == 1 and h == HALVES - 1), is_transpose=True,
                 )
 
-        for step in range(BLOCKS + 1):
-            if step < BLOCKS:
-                square(step)
-            if step >= 1:
-                factor(step - 1)
-            if step == 1:
+        square(0)
+        for j in range(BLOCKS):
+            if j + 1 < BLOCKS:
+                square(j + 1)
+            factor(j)
+            if j == 0:
                 seed_bank(1, "scores0")
 
-        ends = [(c, h, 0, PAIR) for c in range(2) for h in range(HALVES)]
-        for e, (c, h, first, width) in enumerate(ends):
-            logs = sb.tile([P, width], F32, name="logs%d" % e)
-            nc.scalar.activation(logs[:], m_t[c][:, h, first : first + width], ACT.Ln, bias=tiny_col[:])
-            y = sb.tile([P, width], F32, name="y%d" % e)
-            nc.vector.scalar_tensor_tensor(
-                y[:], logs[:], -CAP, n_t[c][:, h, first : first + width], ALU.max, ALU.mult
-            )
-            col = c * PAIR + first
-            nc.sync.dma_start(out[0, h * P : (h + 1) * P, col : col + width], y[:])
+        for c in range(PAIRS):
+            for h in range(HALVES):
+                logs = sb.tile([P, PAIR], F32, name="logs%d" % (HALVES * c + h))
+                nc.scalar.activation(logs[:], m_t[c][:, h, :], ACT.Ln, bias=tiny_col[:])
+                y = sb.tile([P, PAIR], F32, name="y%d" % (HALVES * c + h))
+                nc.vector.scalar_tensor_tensor(y[:], logs[:], -CAP, n_t[c][:, h, :], ALU.max, ALU.mult)
+                nc.sync.dma_start(out[0, h * P : (h + 1) * P, c * PAIR : (c + 1) * PAIR], y[:])

@@ -26,7 +26,7 @@ QUADRANT = 32
 GROUP = SCALE_ROWS * QUADRANT // P
 CAP = 16.0
 BIAS_ROW = P - 1
-SCALE_FIRST = P - SCALE_ROWS
+SCALE_FIRST = P // 2 - SCALE_ROWS
 
 FLOPS = 2 * D * NQ * N
 BYTES = 4 * D * NQ + D * T + SCALE_ROWS * T + 4 * T + 2 * P * (N // 16) + 4 * NQ * N
@@ -40,7 +40,7 @@ def tile_attend_link_focal_topk_kernel(tc, qT, k_words, k_scales, kb, offs, out)
 
         offsets = sb.tile([P, N // 16], U16, name="offsets")
         scale_pool = sb.tile([P, T], U8, name="scale_pool", align_bytes=64)
-        bias_pool = sb.tile([P, T], F32, name="bias_pool")
+        bias_pool = sb.tile([P, T], F32, name="bias_pool", tag="bias_pool", align_bytes=64)
         word_pool = sb.tile([P, T], I32, name="word_pool")
         q_raw = sb.tile([P, PACK, NQ], F32, name="q_raw")
         cap_col = sb.tile([P, 1], F32, name="cap_col")
@@ -50,6 +50,7 @@ def tile_attend_link_focal_topk_kernel(tc, qT, k_words, k_scales, kb, offs, out)
         k_sc = sb.tile([P, N], U8, name="k_sc", align_bytes=64)
 
         nc.vector.memset(scale_pool[:SCALE_FIRST, :].bitcast(I32), 0)
+        nc.vector.memset(scale_pool[P // 2 :, :].bitcast(I32), 0)
         nc.vector.memset(bias_pool[:BIAS_ROW, :].bitcast(I32), 0)
         nc.vector.memset(ident[:], 0.0)
         nc.gpsimd.memset(cap_col[:], -CAP)
@@ -59,9 +60,9 @@ def tile_attend_link_focal_topk_kernel(tc, qT, k_words, k_scales, kb, offs, out)
         words_dram = k_words[0].rearrange("p t r -> p (t r)").bitcast(I32)
         scales_dram = k_scales[0].bitcast(I32)
         nc.sync.dma_start(offsets[:], offs)
-        nc.scalar.dma_start(scale_pool[:].bitcast(I32)[SCALE_FIRST:, :], scales_dram)
-        nc.sync.dma_start(bias_pool[BIAS_ROW:, :], kb[BIAS_ROW:, :])
+        nc.scalar.dma_start(scale_pool[:].bitcast(I32)[SCALE_FIRST : P // 2, :], scales_dram)
         nc.sync.dma_start(q_raw[:], qT[0].rearrange("(p j) w -> p j w", j=PACK))
+        nc.sync.dma_start(bias_pool[BIAS_ROW:, :], kb[BIAS_ROW:, :])
         nc.sync.dma_start(word_pool[:], words_dram)
 
         nc.scalar.activation(floor_col[:], cap_col[:], ACT.Sigmoid)
@@ -88,13 +89,13 @@ def tile_attend_link_focal_topk_kernel(tc, qT, k_words, k_scales, kb, offs, out)
             ACT.Copy,
             scale=-1.0 / CAP,
         )
-        q_codes = sb.tile([P, NQ], U32, name="q_codes", align_bytes=64)
+        q_codes = sb.tile([P, NQ], U32, name="q_codes", tag="bias_pool", align_bytes=64)
         q_sc = sb.tile([P, NQ], U8, name="q_sc", align_bytes=64)
         nc.vector.quantize_mx(
             out=q_codes[:].bitcast(FP8X4), scales=q_sc[:], in_=q_bf[:].rearrange("p w j -> p (w j)")
         )
 
-        bias_t = [ps.tile([P, 2, P], F32, name="bias_t%d" % c, tag="m_t%d" % c) for c in range(PAIRS)]
+        bias_t = [ps.tile([P, 2, P], F32, name="bias_t%d" % c, tag=("m_t0", "scores5")[c]) for c in range(PAIRS)]
         neg_b = sb.tile([P, BLOCKS], F32, name="neg_b")
         knee = sb.tile([P, BLOCKS], F32, name="knee")
         seed = sb.tile([P, BLOCKS], F32, name="seed")
@@ -127,7 +128,7 @@ def tile_attend_link_focal_topk_kernel(tc, qT, k_words, k_scales, kb, offs, out)
                 word_pool[:].bitcast(U32).indirect(offsets[:, PAIR_COLS * c : PAIR_COLS * (c + 1)]),
             )
 
-        parts = [(0, 0, P), (0, P, P)] + [(j, 0, NQ) for j in range(1, BLOCKS)]
+        parts = [(0, 0, P), (0, P, P), (1, 0, NQ), (2, 0, P), (2, P, P), (3, 0, NQ)]
         scores = []
         for u, (j, first, width) in enumerate(parts):
             acc = ps.tile([P, width], F32, name="scores%d" % u, tag="scores%d" % u)
@@ -145,15 +146,20 @@ def tile_attend_link_focal_topk_kernel(tc, qT, k_words, k_scales, kb, offs, out)
         m = [sb.tile([P, NQ], F32, name="m%d" % j) for j in range(BLOCKS)]
         hn = [sb.tile([P, NQ], F32, name="hn%d" % j) for j in range(BLOCKS)]
         nn = [sb.tile([P, NQ], F32, name="nn%d" % j) for j in range(BLOCKS)]
-        m_t = [ps.tile([P, HALVES, PAIR], F32, name="m_t%d" % c, tag="m_t%d" % c) for c in range(PAIRS)]
+        m_t = []
         for u, (j, first, width) in enumerate(parts):
             nc.scalar.activation(
                 m[j][:, first : first + width], scores[u][:], ACT.Sigmoid, bias=neg_b[:, j : j + 1], scale=CAP
             )
-        for j in range(BLOCKS):
-            c, i = divmod(j, 2)
-            for h in range(HALVES):
-                nc.tensor.transpose(m_t[c][:, h, i * P : (i + 1) * P], m[j][:, h * P : (h + 1) * P], ident[:])
+
+        def turn_m(c, tag):
+            bank = ps.tile([P, HALVES, PAIR], F32, name="m_t%d" % c, tag=tag)
+            for i in range(2):
+                for h in range(HALVES):
+                    nc.tensor.transpose(bank[:, h, i * P : (i + 1) * P], m[2 * c + i][:, h * P : (h + 1) * P], ident[:])
+            m_t.append(bank)
+
+        turn_m(0, "m_t0")
 
         def square(j):
             nc.vector.scalar_tensor_tensor(hn[j][:], m[j][:], 2.0, m[j][:], ALU.subtract, ALU.mult)
@@ -178,7 +184,8 @@ def tile_attend_link_focal_topk_kernel(tc, qT, k_words, k_scales, kb, offs, out)
                 square(j + 1)
             factor(j)
             if j == 0:
-                seed_bank(1, "scores0")
+                turn_m(1, "scores0")
+                seed_bank(1, "scores1")
 
         for c in range(PAIRS):
             for h in range(HALVES):

@@ -26,7 +26,7 @@ QUADRANT = 32
 GROUP = SCALE_ROWS * QUADRANT // P
 CAP = 16.0
 BIAS_ROW = P - 1
-SCALE_FIRST = P // 2 - SCALE_ROWS
+SCALE_FIRST = P - SCALE_ROWS
 
 FLOPS = 2 * D * NQ * N
 BYTES = 4 * D * NQ + D * T + SCALE_ROWS * T + 4 * T + 2 * P * (N // 16) + 4 * NQ * N
@@ -50,7 +50,6 @@ def tile_attend_link_focal_topk_kernel(tc, qT, k_words, k_scales, kb, offs, out)
         k_sc = sb.tile([P, N], U8, name="k_sc", align_bytes=64)
 
         nc.vector.memset(scale_pool[:SCALE_FIRST, :].bitcast(I32), 0)
-        nc.vector.memset(scale_pool[P // 2 :, :].bitcast(I32), 0)
         nc.vector.memset(bias_pool[:BIAS_ROW, :].bitcast(I32), 0)
         nc.vector.memset(ident[:], 0.0)
         nc.gpsimd.memset(cap_col[:], -CAP)
@@ -60,7 +59,7 @@ def tile_attend_link_focal_topk_kernel(tc, qT, k_words, k_scales, kb, offs, out)
         words_dram = k_words[0].rearrange("p t r -> p (t r)").bitcast(I32)
         scales_dram = k_scales[0].bitcast(I32)
         nc.sync.dma_start(offsets[:], offs)
-        nc.scalar.dma_start(scale_pool[:].bitcast(I32)[SCALE_FIRST : P // 2, :], scales_dram)
+        nc.scalar.dma_start(scale_pool[:].bitcast(I32)[SCALE_FIRST:, :], scales_dram)
         nc.sync.dma_start(q_raw[:], qT[0].rearrange("(p j) w -> p j w", j=PACK))
         nc.sync.dma_start(bias_pool[BIAS_ROW:, :], kb[BIAS_ROW:, :])
         nc.sync.dma_start(word_pool[:], words_dram)

@@ -24,6 +24,7 @@ PAIR_COLS = PAIR // 16
 SCALE_ROWS = D // 32
 QUADRANT = 32
 GROUP = SCALE_ROWS * QUADRANT // P
+TINY = 2.0**-46
 CAP = 16.0
 BIAS_ROW = P - 1
 SCALE_FIRST = P - SCALE_ROWS
@@ -160,8 +161,8 @@ def tile_attend_link_focal_topk_kernel(tc, qT, k_words, k_scales, kb, offs, out)
 
         turn_m(0, "m_t0")
 
-        def square(j):
-            nc.vector.scalar_tensor_tensor(hn[j][:], m[j][:], 2.0, m[j][:], ALU.subtract, ALU.mult)
+        def square(j, cols=slice(0, NQ)):
+            nc.vector.scalar_tensor_tensor(hn[j][:, cols], m[j][:, cols], 2.0, m[j][:, cols], ALU.subtract, ALU.mult)
 
         def factor(j):
             c, i = divmod(j, 2)
@@ -177,7 +178,8 @@ def tile_attend_link_focal_topk_kernel(tc, qT, k_words, k_scales, kb, offs, out)
                     start=False, stop=(i == 1 and h == HALVES - 1), is_transpose=True,
                 )
 
-        square(0)
+        square(0, slice(0, P))
+        square(0, slice(P, NQ))
         for j in range(BLOCKS):
             if j + 1 < BLOCKS:
                 square(j + 1)
@@ -189,7 +191,7 @@ def tile_attend_link_focal_topk_kernel(tc, qT, k_words, k_scales, kb, offs, out)
         for c in range(PAIRS):
             for h in range(HALVES):
                 logs = sb.tile([P, PAIR], F32, name="logs%d" % (HALVES * c + h))
-                nc.scalar.activation(logs[:], m_t[c][:, h, :], ACT.Ln, bias=tiny_col[:])
+                nc.scalar.activation(logs[:], m_t[c][:, h, :], ACT.Ln, bias=tiny_col[:] if c + h == 0 else TINY)
                 y = sb.tile([P, PAIR], F32, name="y%d" % (HALVES * c + h))
                 nc.vector.scalar_tensor_tensor(y[:], logs[:], -CAP, n_t[c][:, h, :], ALU.max, ALU.mult)
                 nc.sync.dma_start(out[0, h * P : (h + 1) * P, c * PAIR : (c + 1) * PAIR], y[:])

@@ -21,6 +21,7 @@ HALVES = NQ // P
 PAIR = 2 * P
 PAIRS = N // PAIR
 PAIR_COLS = PAIR // 16
+BLOCK_COLS = P // 16
 SCALE_ROWS = D // 32
 QUADRANT = 32
 GROUP = SCALE_ROWS * QUADRANT // P
@@ -48,25 +49,31 @@ def tile_attend_link_focal_topk_kernel(tc, qT, k_words, k_scales, kb, offs, out)
         floor_col = sb.tile([P, 1], F32, name="floor_col")
         tiny_col = sb.tile([P, 1], F32, name="tiny_col")
         ident = sb.tile([P, P], F32, name="ident")
-        k_sc = sb.tile([P, N], U8, name="k_sc", align_bytes=64)
 
         nc.vector.memset(scale_pool[:SCALE_FIRST, :].bitcast(I32), 0)
         nc.vector.memset(bias_pool[:BIAS_ROW, :].bitcast(I32), 0)
         nc.vector.memset(ident[:], 0.0)
-        nc.gpsimd.memset(cap_col[:], -CAP)
+        k_sc = sb.tile([P, N], U8, name="k_sc", align_bytes=64)
         nc.vector.memset(k_sc[:].bitcast(I32), 0)
+        nc.gpsimd.memset(cap_col[:], -CAP)
         make_identity(nc, ident[:], nomemset=True)
 
         words_dram = k_words[0].rearrange("p t r -> p (t r)").bitcast(I32)
         scales_dram = k_scales[0].bitcast(I32)
         nc.sync.dma_start(offsets[:], offs)
         nc.scalar.dma_start(scale_pool[:].bitcast(I32)[SCALE_FIRST:, :], scales_dram)
-        nc.sync.dma_start(q_raw[:], qT[0].rearrange("(p j) w -> p j w", j=PACK))
         nc.sync.dma_start(bias_pool[BIAS_ROW:, :], kb[BIAS_ROW:, :])
+        nc.sync.dma_start(q_raw[:], qT[0].rearrange("(p j) w -> p j w", j=PACK))
         nc.sync.dma_start(word_pool[:], words_dram)
 
         nc.scalar.activation(floor_col[:], cap_col[:], ACT.Sigmoid)
         nc.scalar.activation(tiny_col[:], floor_col[:], ACT.Square)
+
+        bias_g = [sb.tile([P, PAIR], F32, name="bias_g%d" % c) for c in range(PAIRS)]
+        for c in range(PAIRS):
+            nc.scalar.activation(
+                bias_g[c][:], bias_pool[:].indirect(offsets[:, PAIR_COLS * c : PAIR_COLS * (c + 1)]), ACT.Copy
+            )
 
         scale_g = sb.tile([P, N], U8, name="scale_g", align_bytes=64)
         nc.vector.tensor_copy(scale_g[:], scale_pool[:].indirect(offsets[:]))
@@ -76,36 +83,28 @@ def tile_attend_link_focal_topk_kernel(tc, qT, k_words, k_scales, kb, offs, out)
                 scale_g[:].bitcast(I32)[SCALE_FIRST + r : SCALE_FIRST + SCALE_ROWS : GROUP, :],
             )
 
-        bias_g = [sb.tile([P, PAIR], F32, name="bias_g%d" % c) for c in range(PAIRS)]
-        for c in range(PAIRS):
-            nc.vector.tensor_copy(
-                bias_g[c][:], bias_pool[:].indirect(offsets[:, PAIR_COLS * c : PAIR_COLS * (c + 1)])
-            )
-
         q_bf = sb.tile([P, NQ, PACK], BF16, name="q_bf", align_bytes=64)
-        nc.scalar.activation(
+        nc.vector.tensor_scalar(
             q_bf[:].rearrange("p (c i) j -> p c j i", i=PACK),
             q_raw[:].rearrange("p j (c i) -> p c j i", i=PACK),
-            ACT.Copy,
-            scale=-1.0 / CAP,
+            -1.0 / CAP, None, ALU.mult,
         )
-        q_codes = sb.tile([P, NQ], U32, name="q_codes", tag="bias_pool", align_bytes=64)
+        q_codes = sb.tile([P, NQ], U32, name="q_codes", align_bytes=64)
         q_sc = sb.tile([P, NQ], U8, name="q_sc", align_bytes=64)
         nc.vector.quantize_mx(
             out=q_codes[:].bitcast(FP8X4), scales=q_sc[:], in_=q_bf[:].rearrange("p w j -> p (w j)")
         )
 
-        bias_t = [ps.tile([P, 2, P], F32, name="bias_t%d" % c, tag=("m_t0", "scores5")[c]) for c in range(PAIRS)]
+        bias_t = ps.tile([P, BLOCKS, P], F32, name="bias_t", tag="scores0")
         neg_b = sb.tile([P, BLOCKS], F32, name="neg_b")
         knee = sb.tile([P, BLOCKS], F32, name="knee")
         seed = sb.tile([P, BLOCKS], F32, name="seed")
-        for c in range(PAIRS):
-            for i in range(2):
-                nc.tensor.transpose(bias_t[c][:, i, :], bias_g[c][:, i * P : (i + 1) * P], ident[:])
-        for c in range(PAIRS):
-            nc.scalar.activation(seed[:, 2 * c : 2 * c + 2], bias_t[c][:, :, BIAS_ROW], ACT.Copy, scale=-1.0 / CAP)
-            nc.scalar.activation(neg_b[:, 2 * c : 2 * c + 2], bias_t[c][:, :, BIAS_ROW], ACT.Copy, scale=-1.0)
-        nc.scalar.activation(knee[:], seed[:], ACT.Copy, scale=-1.0, bias=-1.0)
+        for j in range(BLOCKS):
+            c, i = divmod(j, 2)
+            nc.tensor.transpose(bias_t[:, j, :], bias_g[c][:, i * P : (i + 1) * P], ident[:])
+        nc.scalar.activation(seed[:], bias_t[:, :, BIAS_ROW], ACT.Copy, scale=-1.0 / CAP)
+        nc.scalar.activation(neg_b[:], bias_t[:, :, BIAS_ROW], ACT.Copy, scale=-1.0)
+        nc.scalar.activation(knee[:], bias_t[:, :, BIAS_ROW], ACT.Copy, scale=1.0 / CAP, bias=-1.0)
 
         n_t = []
 
@@ -120,15 +119,16 @@ def tile_attend_link_focal_topk_kernel(tc, qT, k_words, k_scales, kb, offs, out)
             n_t.append(bank)
 
         seed_bank(0, "n_t0")
+        seed_bank(1, "n_t1")
 
         k_codes = sb.tile([P, N], U32, name="k_codes", align_bytes=64)
-        for c in range(PAIRS):
+        for j in range(BLOCKS):
             nc.vector.tensor_copy(
-                k_codes[:, c * PAIR : (c + 1) * PAIR],
-                word_pool[:].bitcast(U32).indirect(offsets[:, PAIR_COLS * c : PAIR_COLS * (c + 1)]),
+                k_codes[:, j * P : (j + 1) * P],
+                word_pool[:].bitcast(U32).indirect(offsets[:, BLOCK_COLS * j : BLOCK_COLS * (j + 1)]),
             )
 
-        parts = [(0, 0, P), (0, P, P), (1, 0, NQ), (2, 0, P), (2, P, P), (3, 0, NQ)]
+        parts = [(0, 0, P), (0, P, P), (1, 0, NQ), (2, 0, NQ), (3, 0, NQ)]
         scores = []
         for u, (j, first, width) in enumerate(parts):
             acc = ps.tile([P, width], F32, name="scores%d" % u, tag="scores%d" % u)
@@ -161,8 +161,8 @@ def tile_attend_link_focal_topk_kernel(tc, qT, k_words, k_scales, kb, offs, out)
 
         turn_m(0, "m_t0")
 
-        def square(j, cols=slice(0, NQ)):
-            nc.vector.scalar_tensor_tensor(hn[j][:, cols], m[j][:, cols], 2.0, m[j][:, cols], ALU.subtract, ALU.mult)
+        def square(j):
+            nc.vector.scalar_tensor_tensor(hn[j][:], m[j][:], 2.0, m[j][:], ALU.subtract, ALU.mult)
 
         def factor(j):
             c, i = divmod(j, 2)
@@ -178,15 +178,13 @@ def tile_attend_link_focal_topk_kernel(tc, qT, k_words, k_scales, kb, offs, out)
                     start=False, stop=(i == 1 and h == HALVES - 1), is_transpose=True,
                 )
 
-        square(0, slice(0, P))
-        square(0, slice(P, NQ))
+        square(0)
         for j in range(BLOCKS):
             if j + 1 < BLOCKS:
                 square(j + 1)
             factor(j)
             if j == 0:
                 turn_m(1, "scores0")
-                seed_bank(1, "scores1")
 
         for c in range(PAIRS):
             for h in range(HALVES):

@@ -50,9 +50,9 @@ def tile_attend_link_focal_topk_kernel(tc, qT, k_words, k_scales, kb, offs, out)
         tiny_col = sb.tile([P, 1], F32, name="tiny_col")
         ident = sb.tile([P, P], F32, name="ident")
 
+        nc.vector.memset(ident[:], 0.0)
         nc.vector.memset(scale_pool[:SCALE_FIRST, :].bitcast(I32), 0)
         nc.vector.memset(bias_pool[:BIAS_ROW, :].bitcast(I32), 0)
-        nc.vector.memset(ident[:], 0.0)
         k_sc = sb.tile([P, N], U8, name="k_sc", align_bytes=64)
         nc.vector.memset(k_sc[:].bitcast(I32), 0)
         nc.gpsimd.memset(cap_col[:], -CAP)
@@ -95,16 +95,17 @@ def tile_attend_link_focal_topk_kernel(tc, qT, k_words, k_scales, kb, offs, out)
             out=q_codes[:].bitcast(FP8X4), scales=q_sc[:], in_=q_bf[:].rearrange("p w j -> p (w j)")
         )
 
-        bias_t = ps.tile([P, BLOCKS, P], F32, name="bias_t", tag="scores0")
+        bias_t = [ps.tile([P, 2, P], F32, name="bias_t%d" % c, tag=("scores0", "scores3")[c]) for c in range(PAIRS)]
         neg_b = sb.tile([P, BLOCKS], F32, name="neg_b")
         knee = sb.tile([P, BLOCKS], F32, name="knee")
         seed = sb.tile([P, BLOCKS], F32, name="seed")
-        for j in range(BLOCKS):
-            c, i = divmod(j, 2)
-            nc.tensor.transpose(bias_t[:, j, :], bias_g[c][:, i * P : (i + 1) * P], ident[:])
-        nc.scalar.activation(seed[:], bias_t[:, :, BIAS_ROW], ACT.Copy, scale=-1.0 / CAP)
-        nc.scalar.activation(neg_b[:], bias_t[:, :, BIAS_ROW], ACT.Copy, scale=-1.0)
-        nc.scalar.activation(knee[:], bias_t[:, :, BIAS_ROW], ACT.Copy, scale=1.0 / CAP, bias=-1.0)
+        for c in range(PAIRS):
+            for i in range(2):
+                nc.tensor.transpose(bias_t[c][:, i, :], bias_g[c][:, i * P : (i + 1) * P], ident[:])
+        for c in range(PAIRS):
+            nc.scalar.activation(seed[:, 2 * c : 2 * c + 2], bias_t[c][:, :, BIAS_ROW], ACT.Copy, scale=-1.0 / CAP)
+        nc.scalar.activation(neg_b[:], seed[:], ACT.Copy, scale=CAP)
+        nc.scalar.activation(knee[:], seed[:], ACT.Copy, scale=-1.0, bias=-1.0)
 
         n_t = []
 
@@ -119,7 +120,6 @@ def tile_attend_link_focal_topk_kernel(tc, qT, k_words, k_scales, kb, offs, out)
             n_t.append(bank)
 
         seed_bank(0, "n_t0")
-        seed_bank(1, "n_t1")
 
         k_codes = sb.tile([P, N], U32, name="k_codes", align_bytes=64)
         for j in range(BLOCKS):
@@ -184,7 +184,8 @@ def tile_attend_link_focal_topk_kernel(tc, qT, k_words, k_scales, kb, offs, out)
                 square(j + 1)
             factor(j)
             if j == 0:
-                turn_m(1, "scores0")
+                seed_bank(1, "scores0")
+                turn_m(1, "m_t1")
 
         for c in range(PAIRS):
             for h in range(HALVES):

@@ -47,7 +47,6 @@ def tile_attend_link_focal_topk_kernel(tc, qT, k_words, k_scales, kb, offs, out)
         q_raw = sb.tile([P, PACK, NQ], F32, name="q_raw")
         cap_col = sb.tile([P, 1], F32, name="cap_col")
         floor_col = sb.tile([P, 1], F32, name="floor_col")
-        tiny_col = sb.tile([P, 1], F32, name="tiny_col")
         ident = sb.tile([P, P], F32, name="ident")
 
         nc.vector.memset(ident[:], 0.0)
@@ -67,13 +66,6 @@ def tile_attend_link_focal_topk_kernel(tc, qT, k_words, k_scales, kb, offs, out)
         nc.sync.dma_start(word_pool[:], words_dram)
 
         nc.scalar.activation(floor_col[:], cap_col[:], ACT.Sigmoid)
-        nc.scalar.activation(tiny_col[:], floor_col[:], ACT.Square)
-
-        bias_g = [sb.tile([P, PAIR], F32, name="bias_g%d" % c) for c in range(PAIRS)]
-        for c in range(PAIRS):
-            nc.scalar.activation(
-                bias_g[c][:], bias_pool[:].indirect(offsets[:, PAIR_COLS * c : PAIR_COLS * (c + 1)]), ACT.Copy
-            )
 
         scale_g = sb.tile([P, N], U8, name="scale_g", align_bytes=64)
         nc.vector.tensor_copy(scale_g[:], scale_pool[:].indirect(offsets[:]))
@@ -99,13 +91,28 @@ def tile_attend_link_focal_topk_kernel(tc, qT, k_words, k_scales, kb, offs, out)
         neg_b = sb.tile([P, BLOCKS], F32, name="neg_b")
         knee = sb.tile([P, BLOCKS], F32, name="knee")
         seed = sb.tile([P, BLOCKS], F32, name="seed")
-        for c in range(PAIRS):
-            for i in range(2):
-                nc.tensor.transpose(bias_t[c][:, i, :], bias_g[c][:, i * P : (i + 1) * P], ident[:])
-        for c in range(PAIRS):
+
+        def gather_bias(first, count, tag):
+            tile = sb.tile([P, count * P], F32, name="bias_g%d" % first, tag=tag)
+            nc.scalar.activation(
+                tile[:], bias_pool[:].indirect(offsets[:, BLOCK_COLS * first : BLOCK_COLS * (first + count)]), ACT.Copy
+            )
+            for i in range(count):
+                j = first + i
+                nc.tensor.transpose(bias_t[j // 2][:, j % 2, :], tile[:, i * P : (i + 1) * P], ident[:])
+
+        def bias_columns(c):
             nc.scalar.activation(seed[:, 2 * c : 2 * c + 2], bias_t[c][:, :, BIAS_ROW], ACT.Copy, scale=-1.0 / CAP)
-        nc.scalar.activation(neg_b[:], seed[:], ACT.Copy, scale=CAP)
+            nc.scalar.activation(neg_b[:, 2 * c : 2 * c + 2], bias_t[c][:, :, BIAS_ROW], ACT.Copy, scale=-1.0)
+
+        gather_bias(0, 2, "bias_g0")
+        gather_bias(2, 1, "bias_g2")
+        bias_columns(0)
+        gather_bias(3, 1, "bias_g0")
+        bias_columns(1)
         nc.scalar.activation(knee[:], seed[:], ACT.Copy, scale=-1.0, bias=-1.0)
+        tiny_col = sb.tile([P, 1], F32, name="tiny_col", tag="bias_pool", align_bytes=64)
+        nc.scalar.activation(tiny_col[:], floor_col[:], ACT.Square)
 
         n_t = []
 

@@ -194,10 +194,19 @@ def tile_attend_link_focal_topk_kernel(tc, qT, k_words, k_scales, kb, offs, out)
                 seed_bank(1, "scores0")
                 turn_m(1, "m_t1")
 
+        stores = [[(0, PAIR)], [(0, PAIR)], [(0, PAIR)], [(0, PAIR)]]
+        y = [sb.tile([P, PAIR], F32, name="y%d" % u) for u in range(PAIRS * HALVES)]
         for c in range(PAIRS):
             for h in range(HALVES):
-                logs = sb.tile([P, PAIR], F32, name="logs%d" % (HALVES * c + h))
-                nc.scalar.activation(logs[:], m_t[c][:, h, :], ACT.Ln, bias=tiny_col[:] if c + h == 0 else TINY)
-                y = sb.tile([P, PAIR], F32, name="y%d" % (HALVES * c + h))
-                nc.vector.scalar_tensor_tensor(y[:], logs[:], -CAP, n_t[c][:, h, :], ALU.max, ALU.mult)
-                nc.sync.dma_start(out[0, h * P : (h + 1) * P, c * PAIR : (c + 1) * PAIR], y[:])
+                u = HALVES * c + h
+                for i in range(2):
+                    cols = slice(i * P, (i + 1) * P)
+                    logs = sb.tile([P, P], F32, name="logs%d" % (2 * u + i))
+                    nc.scalar.activation(logs[:], m_t[c][:, h, cols], ACT.Ln, bias=tiny_col[:] if u + i == 0 else TINY)
+                    nc.vector.scalar_tensor_tensor(y[u][:, cols], logs[:], -CAP, n_t[c][:, h, cols], ALU.max, ALU.mult)
+                    for first, width in stores[u]:
+                        if first + width == (i + 1) * P:
+                            nc.sync.dma_start(
+                                out[0, h * P : (h + 1) * P, c * PAIR + first : c * PAIR + first + width],
+                                y[u][:, first : first + width],
+                            )

@@ -61,7 +61,7 @@ def tile_attend_link_focal_topk_kernel(tc, qT, k_words, k_scales, kb, offs, out)
         scales_dram = k_scales[0].bitcast(I32)
         nc.sync.dma_start(offsets[:], offs)
         nc.scalar.dma_start(scale_pool[:].bitcast(I32)[SCALE_FIRST:, :], scales_dram)
-        nc.sync.dma_start(bias_pool[BIAS_ROW:, :], kb[BIAS_ROW:, :])
+        nc.scalar.dma_start(bias_pool[BIAS_ROW:, :], kb[BIAS_ROW:, :])
         nc.sync.dma_start(q_raw[:], qT[0].rearrange("(p j) w -> p j w", j=PACK))
         nc.sync.dma_start(word_pool[:], words_dram)
 
@@ -111,7 +111,7 @@ def tile_attend_link_focal_topk_kernel(tc, qT, k_words, k_scales, kb, offs, out)
         gather_bias(3, 1, "bias_g0")
         bias_columns(1)
         nc.scalar.activation(knee[:], seed[:], ACT.Copy, scale=-1.0, bias=-1.0)
-        tiny_col = sb.tile([P, 1], F32, name="tiny_col", tag="bias_pool", align_bytes=64)
+        tiny_col = sb.tile([P, 1], F32, name="tiny_col", tag="bias_g2")
         nc.scalar.activation(tiny_col[:], floor_col[:], ACT.Square)
 
         n_t = []
@@ -128,7 +128,7 @@ def tile_attend_link_focal_topk_kernel(tc, qT, k_words, k_scales, kb, offs, out)
 
         seed_bank(0, "n_t0")
 
-        k_codes = sb.tile([P, N], U32, name="k_codes", align_bytes=64)
+        k_codes = sb.tile([P, N], U32, name="k_codes", tag="bias_pool", align_bytes=64)
         for j in range(BLOCKS):
             nc.vector.tensor_copy(
                 k_codes[:, j * P : (j + 1) * P],

@@ -76,16 +76,21 @@ def tile_attend_link_focal_topk_kernel(tc, qT, k_words, k_scales, kb, offs, out)
             )
 
         q_bf = sb.tile([P, NQ, PACK], BF16, name="q_bf", align_bytes=64)
-        nc.vector.tensor_scalar(
-            q_bf[:].rearrange("p (c i) j -> p c j i", i=PACK),
-            q_raw[:].rearrange("p j (c i) -> p c j i", i=PACK),
-            -1.0 / CAP, None, ALU.mult,
-        )
         q_codes = sb.tile([P, NQ], U32, name="q_codes", align_bytes=64)
         q_sc = sb.tile([P, NQ], U8, name="q_sc", align_bytes=64)
-        nc.vector.quantize_mx(
-            out=q_codes[:].bitcast(FP8X4), scales=q_sc[:], in_=q_bf[:].rearrange("p w j -> p (w j)")
-        )
+        for h in range(HALVES):
+            cols = slice(h * P, (h + 1) * P)
+            nc.vector.tensor_scalar(
+                q_bf[:, cols, :].rearrange("p (c i) j -> p c j i", i=PACK),
+                q_raw[:, :, cols].rearrange("p j (c i) -> p c j i", i=PACK),
+                -1.0 / CAP, None, ALU.mult,
+            )
+        for h in range(HALVES):
+            cols = slice(h * P, (h + 1) * P)
+            nc.vector.quantize_mx(
+                out=q_codes[:, cols].bitcast(FP8X4), scales=q_sc[:, cols],
+                in_=q_bf[:, cols, :].rearrange("p w j -> p (w j)"),
+            )
 
         bias_t = [ps.tile([P, 2, P], F32, name="bias_t%d" % c, tag=("scores0", "scores3")[c]) for c in range(PAIRS)]
         neg_b = sb.tile([P, BLOCKS], F32, name="neg_b")
@@ -114,19 +119,18 @@ def tile_attend_link_focal_topk_kernel(tc, qT, k_words, k_scales, kb, offs, out)
         tiny_col = sb.tile([P, 1], F32, name="tiny_col", tag="bias_g2")
         nc.scalar.activation(tiny_col[:], floor_col[:], ACT.Square)
 
-        n_t = []
+        n_t = {}
 
-        def seed_bank(c, tag):
-            bank = ps.tile([P, HALVES, PAIR], F32, name="n_t%d" % c, tag=tag)
-            for i in range(2):
-                for h in range(HALVES):
-                    nc.tensor.matmul(
-                        bank[:, h, i * P : (i + 1) * P], seed[:, 2 * c + i : 2 * c + i + 1].to_broadcast([P, P]),
-                        ident[:], start=(i == 0 and h == 0), stop=False, is_transpose=True,
-                    )
-            n_t.append(bank)
+        def seed_bank(pieces, tag):
+            bank = ps.tile([P, len(pieces), P], F32, name="n_t%d%d" % pieces[0], tag=tag)
+            for i, (j, h) in enumerate(pieces):
+                nc.tensor.matmul(
+                    bank[:, i, :], seed[:, j : j + 1].to_broadcast([P, P]), ident[:],
+                    start=(i == 0), stop=False, is_transpose=True,
+                )
+                n_t[j, h] = (bank[:, i, :], i == len(pieces) - 1)
 
-        seed_bank(0, "n_t0")
+        seed_bank([(0, 0), (0, 1), (1, 0), (1, 1)], "n_t0")
 
         k_codes = sb.tile([P, N], U32, name="k_codes", tag="bias_pool", align_bytes=64)
         for j in range(BLOCKS):
@@ -172,7 +176,6 @@ def tile_attend_link_focal_topk_kernel(tc, qT, k_words, k_scales, kb, offs, out)
             nc.vector.scalar_tensor_tensor(hn[j][:], m[j][:], 2.0, m[j][:], ALU.subtract, ALU.mult)
 
         def factor(j):
-            c, i = divmod(j, 2)
             for u, (block, first, width) in enumerate(parts):
                 if block == j:
                     nc.vector.scalar_tensor_tensor(
@@ -180,9 +183,9 @@ def tile_attend_link_focal_topk_kernel(tc, qT, k_words, k_scales, kb, offs, out)
                         hn[j][:, first : first + width], ALU.min, ALU.subtract,
                     )
             for h in range(HALVES):
+                target, closes = n_t[j, h]
                 nc.tensor.matmul(
-                    n_t[c][:, h, i * P : (i + 1) * P], nn[j][:, h * P : (h + 1) * P], ident[:],
-                    start=False, stop=(i == 1 and h == HALVES - 1), is_transpose=True,
+                    target, nn[j][:, h * P : (h + 1) * P], ident[:], start=False, stop=closes, is_transpose=True
                 )
 
         square(0)
@@ -191,8 +194,11 @@ def tile_attend_link_focal_topk_kernel(tc, qT, k_words, k_scales, kb, offs, out)
                 square(j + 1)
             factor(j)
             if j == 0:
-                seed_bank(1, "scores0")
+                seed_bank([(2, 0), (2, 1)], "scores0")
                 turn_m(1, "m_t1")
+            if j == 1:
+                seed_bank([(3, 0)], "scores2")
+                seed_bank([(3, 1)], "scores1")
 
         stores = [[(0, PAIR)], [(0, PAIR)], [(0, PAIR)], [(0, PAIR)]]
         y = [sb.tile([P, PAIR], F32, name="y%d" % u) for u in range(PAIRS * HALVES)]
@@ -203,7 +209,7 @@ def tile_attend_link_focal_topk_kernel(tc, qT, k_words, k_scales, kb, offs, out)
                     cols = slice(i * P, (i + 1) * P)
                     logs = sb.tile([P, P], F32, name="logs%d" % (2 * u + i))
                     nc.scalar.activation(logs[:], m_t[c][:, h, cols], ACT.Ln, bias=tiny_col[:] if u + i == 0 else TINY)
-                    nc.vector.scalar_tensor_tensor(y[u][:, cols], logs[:], -CAP, n_t[c][:, h, cols], ALU.max, ALU.mult)
+                    nc.vector.scalar_tensor_tensor(y[u][:, cols], logs[:], -CAP, n_t[2 * c + i, h][0], ALU.max, ALU.mult)
                     for first, width in stores[u]:
                         if first + width == (i + 1) * P:
                             nc.sync.dma_start(

@@ -173,7 +173,10 @@ def tile_attend_link_focal_topk_kernel(tc, qT, k_words, k_scales, kb, offs, out)
         turn_m(0, "m_t0")
 
         def square(j):
-            nc.vector.scalar_tensor_tensor(hn[j][:], m[j][:], 2.0, m[j][:], ALU.subtract, ALU.mult)
+            for block, first, width in parts:
+                if block == j:
+                    cols = slice(first, first + width)
+                    nc.vector.scalar_tensor_tensor(hn[j][:, cols], m[j][:, cols], 2.0, m[j][:, cols], ALU.subtract, ALU.mult)
 
         def factor(j):
             for u, (block, first, width) in enumerate(parts):
@@ -189,16 +192,16 @@ def tile_attend_link_focal_topk_kernel(tc, qT, k_words, k_scales, kb, offs, out)
                 )
 
         square(0)
-        for j in range(BLOCKS):
-            if j + 1 < BLOCKS:
-                square(j + 1)
-            factor(j)
-            if j == 0:
-                seed_bank([(2, 0), (2, 1)], "scores0")
-                turn_m(1, "m_t1")
-            if j == 1:
-                seed_bank([(3, 0)], "scores2")
-                seed_bank([(3, 1)], "scores1")
+        factor(0)
+        seed_bank([(2, 0), (2, 1)], "scores0")
+        seed_bank([(3, 0), (3, 1)], "scores1")
+        square(1)
+        square(2)
+        factor(1)
+        turn_m(1, "scores2")
+        square(3)
+        factor(2)
+        factor(3)
 
         stores = [[(0, PAIR)], [(0, PAIR)], [(0, PAIR)], [(0, PAIR)]]
         y = [sb.tile([P, PAIR], F32, name="y%d" % u) for u in range(PAIRS * HALVES)]

@@ -28,7 +28,7 @@ GROUP = SCALE_ROWS * QUADRANT // P
 TINY = 2.0**-46
 CAP = 16.0
 BIAS_ROW = P - 1
-SCALE_FIRST = P - SCALE_ROWS
+SCALE_FIRST = P // 2 - SCALE_ROWS
 
 FLOPS = 2 * D * NQ * N
 BYTES = 4 * D * NQ + D * T + SCALE_ROWS * T + 4 * T + 2 * P * (N // 16) + 4 * NQ * N
@@ -49,9 +49,10 @@ def tile_attend_link_focal_topk_kernel(tc, qT, k_words, k_scales, kb, offs, out)
         floor_col = sb.tile([P, 1], F32, name="floor_col")
         ident = sb.tile([P, P], F32, name="ident")
 
-        nc.vector.memset(ident[:], 0.0)
-        nc.vector.memset(scale_pool[:SCALE_FIRST, :].bitcast(I32), 0)
         nc.vector.memset(bias_pool[:BIAS_ROW, :].bitcast(I32), 0)
+        nc.vector.memset(scale_pool[:SCALE_FIRST, :].bitcast(I32), 0)
+        nc.vector.memset(scale_pool[P // 2 :, :].bitcast(I32), 0)
+        nc.vector.memset(ident[:], 0.0)
         k_sc = sb.tile([P, N], U8, name="k_sc", align_bytes=64)
         nc.vector.memset(k_sc[:].bitcast(I32), 0)
         nc.gpsimd.memset(cap_col[:], -CAP)
@@ -60,7 +61,7 @@ def tile_attend_link_focal_topk_kernel(tc, qT, k_words, k_scales, kb, offs, out)
         words_dram = k_words[0].rearrange("p t r -> p (t r)").bitcast(I32)
         scales_dram = k_scales[0].bitcast(I32)
         nc.sync.dma_start(offsets[:], offs)
-        nc.scalar.dma_start(scale_pool[:].bitcast(I32)[SCALE_FIRST:, :], scales_dram)
+        nc.scalar.dma_start(scale_pool[:].bitcast(I32)[SCALE_FIRST : P // 2, :], scales_dram)
         nc.scalar.dma_start(bias_pool[BIAS_ROW:, :], kb[BIAS_ROW:, :])
         nc.sync.dma_start(q_raw[:], qT[0].rearrange("(p j) w -> p j w", j=PACK))
         nc.sync.dma_start(word_pool[:], words_dram)

@@ -96,7 +96,7 @@ def tile_attend_link_focal_topk_kernel(tc, qT, k_words, k_scales, kb, offs, out)
         bias_t = [ps.tile([P, 2, P], F32, name="bias_t%d" % c, tag=("scores0", "scores3")[c]) for c in range(PAIRS)]
         neg_b = sb.tile([P, BLOCKS], F32, name="neg_b")
         knee = sb.tile([P, BLOCKS], F32, name="knee")
-        seed = sb.tile([P, BLOCKS], F32, name="seed")
+        seed = sb.tile([P, 2], F32, name="seed")
 
         def gather_bias(first, count, tag):
             tile = sb.tile([P, count * P], F32, name="bias_g%d" % first, tag=tag)
@@ -107,26 +107,23 @@ def tile_attend_link_focal_topk_kernel(tc, qT, k_words, k_scales, kb, offs, out)
                 j = first + i
                 nc.tensor.transpose(bias_t[j // 2][:, j % 2, :], tile[:, i * P : (i + 1) * P], ident[:])
 
-        def bias_columns(c):
-            nc.scalar.activation(seed[:, 2 * c : 2 * c + 2], bias_t[c][:, :, BIAS_ROW], ACT.Copy, scale=-1.0 / CAP)
-            nc.scalar.activation(neg_b[:, 2 * c : 2 * c + 2], bias_t[c][:, :, BIAS_ROW], ACT.Copy, scale=-1.0)
-
         gather_bias(0, 2, "bias_g0")
         gather_bias(2, 1, "bias_g2")
-        bias_columns(0)
+        nc.scalar.activation(seed[:, :2], bias_t[0][:, :, BIAS_ROW], ACT.Copy, scale=-1.0 / CAP)
+        nc.scalar.activation(neg_b[:, :2], bias_t[0][:, :, BIAS_ROW], ACT.Copy, scale=-1.0)
         gather_bias(3, 1, "bias_g0")
-        bias_columns(1)
-        nc.scalar.activation(knee[:], seed[:], ACT.Copy, scale=-1.0, bias=-1.0)
-        tiny_col = sb.tile([P, 1], F32, name="tiny_col", tag="bias_g2")
-        nc.scalar.activation(tiny_col[:], floor_col[:], ACT.Square)
+        nc.scalar.activation(neg_b[:, 2:], bias_t[1][:, :, BIAS_ROW], ACT.Copy, scale=-1.0)
+        tiny_col = sb.tile([P, 1], F32, name="tiny_col")
+        nc.gpsimd.tensor_tensor(tiny_col[:], floor_col[:], floor_col[:], ALU.mult)
 
         n_t = {}
+        seeds = [seed]
 
         def seed_bank(pieces, tag):
             bank = ps.tile([P, len(pieces), P], F32, name="n_t%d%d" % pieces[0], tag=tag)
             for i, (j, h) in enumerate(pieces):
                 nc.tensor.matmul(
-                    bank[:, i, :], seed[:, j : j + 1].to_broadcast([P, P]), ident[:],
+                    bank[:, i, :], seeds[j // 2][:, j % 2 : j % 2 + 1].to_broadcast([P, P]), ident[:],
                     start=(i == 0), stop=False, is_transpose=True,
                 )
                 n_t[j, h] = (bank[:, i, :], i == len(pieces) - 1)
@@ -139,6 +136,11 @@ def tile_attend_link_focal_topk_kernel(tc, qT, k_words, k_scales, kb, offs, out)
                 k_codes[:, j * P : (j + 1) * P],
                 word_pool[:].bitcast(U32).indirect(offsets[:, BLOCK_COLS * j : BLOCK_COLS * (j + 1)]),
             )
+
+        late_seed = sb.tile([P, 2], F32, name="late_seed")
+        nc.vector.tensor_scalar(knee[:], neg_b[:], -1.0 / CAP, -1.0, ALU.mult, ALU.add)
+        nc.vector.tensor_scalar(late_seed[:], neg_b[:, 2:], 1.0 / CAP, None, ALU.mult)
+        seeds.append(late_seed)
 
         parts = [(0, 0, P), (0, P, P), (1, 0, NQ), (2, 0, NQ), (3, 0, NQ)]
         scores = []
@@ -212,7 +214,7 @@ def tile_attend_link_focal_topk_kernel(tc, qT, k_words, k_scales, kb, offs, out)
                 for i in range(2):
                     cols = slice(i * P, (i + 1) * P)
                     logs = sb.tile([P, P], F32, name="logs%d" % (2 * u + i))
-                    nc.scalar.activation(logs[:], m_t[c][:, h, cols], ACT.Ln, bias=tiny_col[:] if u + i == 0 else TINY)
+                    nc.scalar.activation(logs[:], m_t[c][:, h, cols], ACT.Ln, bias=tiny_col[:] if (u, i) == (0, 1) else TINY)
                     nc.vector.scalar_tensor_tensor(y[u][:, cols], logs[:], -CAP, n_t[2 * c + i, h][0], ALU.max, ALU.mult)
                     for first, width in stores[u]:
                         if first + width == (i + 1) * P:

@@ -60,10 +60,12 @@ def tile_attend_link_focal_topk_kernel(tc, qT, k_words, k_scales, kb, offs, out)
 
         words_dram = k_words[0].rearrange("p t r -> p (t r)").bitcast(I32)
         scales_dram = k_scales[0].bitcast(I32)
+        q_dram = qT[0].rearrange("(p j) w -> p j w", j=PACK)
+        nc.sync.dma_start(q_raw[:, :1, :], q_dram[:, :1, :])
         nc.sync.dma_start(offsets[:], offs)
         nc.scalar.dma_start(scale_pool[:].bitcast(I32)[SCALE_FIRST : P // 2, :], scales_dram)
         nc.scalar.dma_start(bias_pool[BIAS_ROW:, :], kb[BIAS_ROW:, :])
-        nc.sync.dma_start(q_raw[:], qT[0].rearrange("(p j) w -> p j w", j=PACK))
+        nc.sync.dma_start(q_raw[:, 1:, :], q_dram[:, 1:, :])
         nc.sync.dma_start(word_pool[:], words_dram)
 
         nc.scalar.activation(floor_col[:], cap_col[:], ACT.Sigmoid)

@@ -72,10 +72,11 @@ def tile_attend_link_focal_topk_kernel(tc, qT, k_words, k_scales, kb, offs, out)
 
         scale_g = sb.tile([P, N], U8, name="scale_g", align_bytes=64)
         nc.vector.tensor_copy(scale_g[:], scale_pool[:].indirect(offsets[:]))
-        for r in range(GROUP):
+        whole, first_pair, second_pair = slice(0, N // 4), slice(0, PAIR // 4), slice(PAIR // 4, N // 4)
+        for r, cols in [(0, whole), (1, whole), (2, whole), (3, first_pair), (3, second_pair)]:
             nc.sync.dma_start(
-                k_sc[:].bitcast(I32)[r:P:QUADRANT, :],
-                scale_g[:].bitcast(I32)[SCALE_FIRST + r : SCALE_FIRST + SCALE_ROWS : GROUP, :],
+                k_sc[:].bitcast(I32)[r:P:QUADRANT, cols],
+                scale_g[:].bitcast(I32)[SCALE_FIRST + r : SCALE_FIRST + SCALE_ROWS : GROUP, cols],
             )
 
         q_bf = sb.tile([P, NQ, PACK], BF16, name="q_bf", align_bytes=64)

from contextlib import ExitStack

import concourse.mybir as mybir
from concourse.masks import make_identity

F32 = mybir.dt.float32
BF16 = mybir.dt.bfloat16
I32 = mybir.dt.int32
U32 = mybir.dt.uint32
U16 = mybir.dt.uint16
U8 = mybir.dt.uint8
FP8X4 = mybir.dt.float8_e4m3fn_x4
ACT = mybir.ActivationFunctionType
ALU = mybir.AluOpType

P = 128
PACK = 4
D, T, NQ, N = 512, 2048, 256, 512
BLOCKS = N // P
HALVES = NQ // P
PAIR = 2 * P
PAIRS = N // PAIR
PAIR_COLS = PAIR // 16
BLOCK_COLS = P // 16
SCALE_ROWS = D // 32
QUADRANT = 32
GROUP = SCALE_ROWS * QUADRANT // P
TINY = 2.0**-46
CAP = 16.0
BIAS_ROW = P - 1
SCALE_FIRST = P // 2 - SCALE_ROWS

FLOPS = 2 * D * NQ * N
BYTES = 4 * D * NQ + D * T + SCALE_ROWS * T + 4 * T + 2 * P * (N // 16) + 4 * NQ * N


def tile_attend_link_focal_topk_kernel(tc, qT, k_words, k_scales, kb, offs, out):
    nc = tc.nc
    with ExitStack() as ctx:
        sb = ctx.enter_context(tc.tile_pool(name="sb", bufs=1))
        ps = ctx.enter_context(tc.psum_pool(name="ps", bufs=1))

        offsets = sb.tile([P, N // 16], U16, name="offsets")
        scale_pool = sb.tile([P, T], U8, name="scale_pool", align_bytes=64)
        bias_pool = sb.tile([P, T], F32, name="bias_pool", tag="bias_pool", align_bytes=64)
        word_pool = sb.tile([P, T], I32, name="word_pool")
        q_raw = sb.tile([P, PACK, NQ], F32, name="q_raw")
        cap_col = sb.tile([P, 1], F32, name="cap_col")
        floor_col = sb.tile([P, 1], F32, name="floor_col")
        ident = sb.tile([P, P], F32, name="ident")

        nc.vector.memset(bias_pool[:BIAS_ROW, :].bitcast(I32), 0)
        nc.vector.memset(scale_pool[:SCALE_FIRST, :].bitcast(I32), 0)
        nc.vector.memset(scale_pool[P // 2 :, :].bitcast(I32), 0)
        nc.vector.memset(ident[:], 0.0)
        k_sc = sb.tile([P, N], U8, name="k_sc", align_bytes=64)
        nc.vector.memset(k_sc[:].bitcast(I32), 0)
        nc.gpsimd.memset(cap_col[:], -CAP)
        make_identity(nc, ident[:], nomemset=True)

        words_dram = k_words[0].rearrange("p t r -> p (t r)").bitcast(I32)
        scales_dram = k_scales[0].bitcast(I32)
        q_dram = qT[0].rearrange("(p j) w -> p j w", j=PACK)
        nc.sync.dma_start(q_raw[:, :1, :], q_dram[:, :1, :])
        nc.sync.dma_start(offsets[:], offs)
        nc.scalar.dma_start(scale_pool[:].bitcast(I32)[SCALE_FIRST : P // 2, :], scales_dram)
        nc.scalar.dma_start(bias_pool[BIAS_ROW:, :], kb[BIAS_ROW:, :])
        nc.sync.dma_start(q_raw[:, 1:, :], q_dram[:, 1:, :])
        nc.sync.dma_start(word_pool[:], words_dram)

        nc.scalar.activation(floor_col[:], cap_col[:], ACT.Sigmoid)

        scale_g = sb.tile([P, N], U8, name="scale_g", align_bytes=64)
        nc.vector.tensor_copy(scale_g[:], scale_pool[:].indirect(offsets[:]))
        whole, first_pair, second_pair = slice(0, N // 4), slice(0, PAIR // 4), slice(PAIR // 4, N // 4)
        for r, cols in [(0, whole), (1, whole), (2, whole), (3, first_pair), (3, second_pair)]:
            nc.sync.dma_start(
                k_sc[:].bitcast(I32)[r:P:QUADRANT, cols],
                scale_g[:].bitcast(I32)[SCALE_FIRST + r : SCALE_FIRST + SCALE_ROWS : GROUP, cols],
            )

        q_bf = sb.tile([P, NQ, PACK], BF16, name="q_bf", align_bytes=64)
        q_codes = sb.tile([P, NQ], U32, name="q_codes", align_bytes=64)
        q_sc = sb.tile([P, NQ], U8, name="q_sc", align_bytes=64)
        for h in range(HALVES):
            cols = slice(h * P, (h + 1) * P)
            nc.vector.tensor_scalar(
                q_bf[:, cols, :].rearrange("p (c i) j -> p c j i", i=PACK),
                q_raw[:, :, cols].rearrange("p j (c i) -> p c j i", i=PACK),
                -1.0 / CAP, None, ALU.mult,
            )
        for h in range(HALVES):
            cols = slice(h * P, (h + 1) * P)
            nc.vector.quantize_mx(
                out=q_codes[:, cols].bitcast(FP8X4), scales=q_sc[:, cols],
                in_=q_bf[:, cols, :].rearrange("p w j -> p (w j)"),
            )

        bias_t = [ps.tile([P, 2, P], F32, name="bias_t%d" % c, tag=("scores0", "scores3")[c]) for c in range(PAIRS)]
        neg_b = sb.tile([P, BLOCKS], F32, name="neg_b")
        knee = sb.tile([P, BLOCKS], F32, name="knee")
        seed = sb.tile([P, 2], F32, name="seed")

        def gather_bias(first, count, tag):
            tile = sb.tile([P, count * P], F32, name="bias_g%d" % first, tag=tag)
            nc.scalar.activation(
                tile[:], bias_pool[:].indirect(offsets[:, BLOCK_COLS * first : BLOCK_COLS * (first + count)]), ACT.Copy
            )
            for i in range(count):
                j = first + i
                nc.tensor.transpose(bias_t[j // 2][:, j % 2, :], tile[:, i * P : (i + 1) * P], ident[:])

        gather_bias(0, 2, "bias_g0")
        gather_bias(2, 1, "bias_g2")
        nc.scalar.activation(seed[:, :2], bias_t[0][:, :, BIAS_ROW], ACT.Copy, scale=-1.0 / CAP)
        nc.scalar.activation(neg_b[:, :2], bias_t[0][:, :, BIAS_ROW], ACT.Copy, scale=-1.0)
        gather_bias(3, 1, "bias_g0")
        nc.scalar.activation(neg_b[:, 2:], bias_t[1][:, :, BIAS_ROW], ACT.Copy, scale=-1.0)
        tiny_col = sb.tile([P, 1], F32, name="tiny_col")
        nc.gpsimd.tensor_tensor(tiny_col[:], floor_col[:], floor_col[:], ALU.mult)

        n_t = {}
        seeds = [seed]

        def seed_bank(pieces, tag):
            bank = ps.tile([P, len(pieces), P], F32, name="n_t%d%d" % pieces[0], tag=tag)
            for i, (j, h) in enumerate(pieces):
                nc.tensor.matmul(
                    bank[:, i, :], seeds[j // 2][:, j % 2 : j % 2 + 1].to_broadcast([P, P]), ident[:],
                    start=(i == 0), stop=False, is_transpose=True,
                )
                n_t[j, h] = (bank[:, i, :], i == len(pieces) - 1)

        seed_bank([(0, 0), (0, 1), (1, 0), (1, 1)], "n_t0")

        k_codes = sb.tile([P, N], U32, name="k_codes", tag="bias_pool", align_bytes=64)
        for j in range(BLOCKS):
            nc.vector.tensor_copy(
                k_codes[:, j * P : (j + 1) * P],
                word_pool[:].bitcast(U32).indirect(offsets[:, BLOCK_COLS * j : BLOCK_COLS * (j + 1)]),
            )

        late_seed = sb.tile([P, 2], F32, name="late_seed")
        nc.vector.tensor_scalar(knee[:], neg_b[:], -1.0 / CAP, -1.0, ALU.mult, ALU.add)
        nc.vector.tensor_scalar(late_seed[:], neg_b[:, 2:], 1.0 / CAP, None, ALU.mult)
        seeds.append(late_seed)

        parts = [(0, 0, P), (0, P, P), (1, 0, NQ), (2, 0, NQ), (3, 0, NQ)]
        scores = []
        for u, (j, first, width) in enumerate(parts):
            acc = ps.tile([P, width], F32, name="scores%d" % u, tag="scores%d" % u)
            nc.tensor.matmul_mx(
                out=acc[:],
                lhsT=k_codes[:, j * P : (j + 1) * P].bitcast(FP8X4),
                lhsT_scale=k_sc[:, j * P : (j + 1) * P],
                rhs=q_codes[:, first : first + width].bitcast(FP8X4),
                rhs_scale=q_sc[:, first : first + width],
                start=True,
                stop=True,
            )
            scores.append(acc)

        m = [sb.tile([P, NQ], F32, name="m%d" % j) for j in range(BLOCKS)]
        hn = [sb.tile([P, NQ], F32, name="hn%d" % j) for j in range(BLOCKS)]
        nn = [sb.tile([P, NQ], F32, name="nn%d" % j) for j in range(BLOCKS)]
        m_t = []
        for u, (j, first, width) in enumerate(parts):
            nc.scalar.activation(
                m[j][:, first : first + width], scores[u][:], ACT.Sigmoid, bias=neg_b[:, j : j + 1], scale=CAP
            )

        def turn_m(c, tag):
            bank = ps.tile([P, HALVES, PAIR], F32, name="m_t%d" % c, tag=tag)
            for i in range(2):
                for h in range(HALVES):
                    nc.tensor.transpose(bank[:, h, i * P : (i + 1) * P], m[2 * c + i][:, h * P : (h + 1) * P], ident[:])
            m_t.append(bank)

        turn_m(0, "m_t0")

        def square(j):
            for block, first, width in parts:
                if block == j:
                    cols = slice(first, first + width)
                    nc.vector.scalar_tensor_tensor(hn[j][:, cols], m[j][:, cols], 2.0, m[j][:, cols], ALU.subtract, ALU.mult)

        def factor(j):
            for u, (block, first, width) in enumerate(parts):
                if block == j:
                    nc.vector.scalar_tensor_tensor(
                        nn[j][:, first : first + width], scores[u][:], knee[:, j : j + 1],
                        hn[j][:, first : first + width], ALU.min, ALU.subtract,
                    )
            for h in range(HALVES):
                target, closes = n_t[j, h]
                nc.tensor.matmul(
                    target, nn[j][:, h * P : (h + 1) * P], ident[:], start=False, stop=closes, is_transpose=True
                )

        square(0)
        factor(0)
        seed_bank([(2, 0), (2, 1)], "scores0")
        seed_bank([(3, 0), (3, 1)], "scores1")
        square(1)
        square(2)
        factor(1)
        turn_m(1, "scores2")
        square(3)
        factor(2)
        factor(3)

        stores = [[(0, PAIR)], [(0, PAIR)], [(0, PAIR)], [(0, PAIR)]]
        y = [sb.tile([P, PAIR], F32, name="y%d" % u) for u in range(PAIRS * HALVES)]
        for c in range(PAIRS):
            for h in range(HALVES):
                u = HALVES * c + h
                for i in range(2):
                    cols = slice(i * P, (i + 1) * P)
                    logs = sb.tile([P, P], F32, name="logs%d" % (2 * u + i))
                    nc.scalar.activation(logs[:], m_t[c][:, h, cols], ACT.Ln, bias=tiny_col[:] if (u, i) == (0, 1) else TINY)
                    nc.vector.scalar_tensor_tensor(y[u][:, cols], logs[:], -CAP, n_t[2 * c + i, h][0], ALU.max, ALU.mult)
                    for first, width in stores[u]:
                        if first + width == (i + 1) * P:
                            nc.sync.dma_start(
                                out[0, h * P : (h + 1) * P, c * PAIR + first : c * PAIR + first + width],
                                y[u][:, first : first + width],
                            )
